import numpy as np
import ml_dtypes


def mxq(x, axis, fmt="e4m3"):
    dtype, down = {"e4m3": (ml_dtypes.float8_e4m3fn, 7), "e5m2": (ml_dtypes.float8_e5m2, 14)}[fmt]
    v = np.moveaxis(np.asarray(x, np.float32).astype(ml_dtypes.bfloat16).astype(np.float64), axis, -1)
    blocks = v.reshape(v.shape[:-1] + (-1, 32))
    amax = np.abs(blocks).max(-1, keepdims=True)
    byte = np.maximum(np.where(amax > 0, np.frexp(amax)[1] - 1 + 127, 0) - down, 1)
    scale = np.exp2(byte - 127.0)
    codes = (blocks / scale).astype(np.float32).astype(dtype).astype(np.float64)
    return np.moveaxis((codes * scale).reshape(v.shape), -1, axis)


WIDE = False


def mx_kscale(k):
    if not WIDE:
        return np.ones(k)
    levels = np.array([10, -10, 5, -5, 0])
    if k % 512:
        return np.exp2(np.random.permutation(np.resize(levels, k // 32))).repeat(32)
    a = np.empty((k // 512, 16))
    for p in range(k // 512):
        a[p, :8] = np.random.permutation(np.resize(levels, 8))
        for g in range(8):
            far = levels[np.abs(levels - a[p, g]) >= 10]
            a[p, g + 8] = far[np.random.randint(len(far))]
    return np.exp2(a.ravel()).repeat(32)


def f64(x):
    return np.asarray(x).astype(np.float64)


def striped(idx):
    return np.tile(idx.reshape(-1, 16).T, (8, 1)).astype(np.uint16)


def unstriped(offs):
    return offs[:16].T.reshape(-1).astype(np.int64)


def pack_weight(w):
    k, n = w.shape
    w = f64(np.asarray(w, np.float32).astype(ml_dtypes.bfloat16)).reshape(k // 32, 32, n)
    amax = np.abs(w).max(1)
    byte = np.clip(np.where(amax > 0, np.frexp(amax)[1] - 1 + 127 - 7, 1), 1, 254)
    scaled = (w * np.exp2(127.0 - byte)[:, None, :]).reshape(k, n).astype(np.float32)
    words = np.ascontiguousarray(scaled.reshape(k // 512, 128, 4, n).transpose(0, 1, 3, 2)).astype(ml_dtypes.float8_e4m3fn).view(np.uint8)
    return words, np.ascontiguousarray(byte.astype(np.uint8).reshape(k // 512, 16, n))


def unpack_weight(words, scales):
    g, p, n, _ = words.shape
    vals = np.ascontiguousarray(words).view(ml_dtypes.float8_e4m3fn).astype(np.float64) * np.repeat(np.exp2(scales.astype(np.float64) - 127.0), 8, axis=1)[..., None]
    return vals.transpose(0, 1, 3, 2).reshape(g * 512, n)


def planes(y):
    n, m = y.shape
    v = y.astype(np.float32).astype(ml_dtypes.bfloat16).astype(np.float64).reshape(n // 32, 32, m)
    top = np.abs(v).max(1)
    byte = np.clip(np.where(top > 0, np.frexp(top)[1] - 1 + 127 - 7, 1), 1, 254)
    codes = (v * np.exp2(127.0 - byte)[:, None, :]).reshape(n, m).astype(np.float32).astype(ml_dtypes.float8_e4m3fn).view(np.uint8)
    words = codes.reshape(n // 512, 128, 4, m).transpose(0, 1, 3, 2)
    return np.ascontiguousarray(words), np.ascontiguousarray(byte.astype(np.uint8).reshape(n // 512, 16, m))


def gelu(v):
    return 0.5 * v * (1.0 + np.tanh(np.sqrt(2.0 / np.pi) * (v + 0.044715 * v**3)))


K, T, S, N = 1024, 1024, 512, 512


def setup_inputs():
    n = np.random.standard_normal
    s = mx_kscale(K)[:, None]
    packed_xT = pack_weight(n((K, T)) * s)
    return {
        "x_words": packed_xT[0],
        "x_scales": packed_xT[1],
        "mask": (n((N, T))).astype(np.float32),
        "w1": (n((K, N)) / np.sqrt(K) / s).astype(np.float32),
        "offs": striped(np.random.permutation(T)[:S]),
    }


def reference(x_words, x_scales, mask, w1, offs):
    xq = unpack_weight(x_words, x_scales)[:, unstriped(offs)]
    y = gelu(mxq(f64(w1), 0, "e4m3").T @ xq)
    out = f64(mask).copy()
    out[:, unstriped(offs)] = y
    out_0 = out
    return (out_0,) + planes(out_0)

@@ -1,0 +1,156 @@
+from contextlib import ExitStack
+
+import concourse.mybir as mybir
+
+K, T, S, M = 1024, 1024, 512, 512
+FLOPS = 2 * K * S * M
+
+F32 = mybir.dt.float32
+BF16 = mybir.dt.bfloat16
+I32 = mybir.dt.int32
+U32 = mybir.dt.uint32
+U16 = mybir.dt.uint16
+U8 = mybir.dt.uint8
+FP8X4 = mybir.dt.float8_e4m3fn_x4
+GELU = mybir.ActivationFunctionType.Gelu_apprx_tanh
+
+P = 128
+PACK = 4
+K_PASS = P * PACK
+PASSES = K // K_PASS
+LIST_ROWS = 16
+FIRST_SLICES = ((0, 128), (128, 256), (256, 512))
+OUT_CHUNKS = ((0, 512), (512, 768), (768, 1024))
+
+
+def tile_picked_zmae_lingelu_po_kernel(
+    tc, x_words, x_scales, mask, w1, offs, out_0, out_1, out_2
+):
+    nc = tc.nc
+    with ExitStack() as ctx:
+        keep = ctx.enter_context(tc.tile_pool(name="keep", bufs=1))
+        psum = ctx.enter_context(tc.psum_pool(name="psum", bufs=1))
+
+        offsets = keep.tile([P, S // LIST_ROWS], U16, name="offsets")
+        nc.sync.dma_start(offsets[:], offs)
+
+        def picks(a, b):
+            return offsets[:, a // LIST_ROWS : b // LIST_ROWS]
+
+        scale_table = keep.tile([P, T], U8, name="scale_table", align_bytes=64)
+        nc.gpsimd.memset(scale_table[:].bitcast(I32), 0)
+
+        def load_w(g, a, b):
+            raw = keep.tile([P, PACK, b - a], F32, name=f"w_raw{g}_{a}", align_bytes=64)
+            rows = w1[g * K_PASS : (g + 1) * K_PASS, a:b]
+            nc.sync.dma_start(raw[:], rows.rearrange("(p j) c -> p j c", j=PACK))
+            return raw
+
+        def load_x(g, pieces):
+            table = keep.tile([P, T], U32, name=f"word_table{g}", align_bytes=64)
+            words_in = x_words[g].rearrange("p n t -> p (n t)").bitcast(I32)
+            width = T // pieces
+            for a in range(0, T, width):
+                nc.sync.dma_start(table[:, a : a + width].bitcast(I32), words_in[:, a : a + width])
+            return table
+
+        for q in range(4):
+            nc.sync.dma_start(
+                scale_table[32 * q : 32 * q + 4 * PASSES, :].bitcast(I32),
+                x_scales[:, 4 * q : 4 * q + 4, :].bitcast(I32),
+            )
+        x0 = load_x(0, 2)
+        w0a = load_w(0, 0, M // 2)
+        w0b = load_w(0, M // 2, M)
+        w1a = load_w(1, 0, 384)
+        w1b = load_w(1, 384, M)
+        x1 = load_x(1, 1)
+        mask_rows = mask.rearrange("(p t) c -> p t c", t=PACK)
+        out_rows = out_0.rearrange("(p t) c -> p t c", t=PACK)
+        windows = []
+        for t in range(PACK):
+            window = keep.tile([P, T], F32, name=f"window{t}", align_bytes=64)
+            nc.sync.dma_start(window[:], mask_rows[:, t, :])
+            windows.append(window)
+
+        w_bf = [keep.tile([P, PACK, P, PACK], BF16, name=f"w_bf{g}", align_bytes=64) for g in range(PASSES)]
+        w_codes = [keep.tile([P, M], U32, name=f"w_codes{g}", align_bytes=64) for g in range(PASSES)]
+        w_scales = [keep.tile([P, M], U8, name=f"w_scales{g}", align_bytes=64) for g in range(PASSES)]
+
+        def cast_w(copy, g, raw, raw0, a, b):
+            copy(
+                w_bf[g][:, :, a:b, :].rearrange("p t m j -> p m j t"),
+                raw[:, :, PACK * (a - raw0) : PACK * (b - raw0)].rearrange("p j (m t) -> p m j t", t=PACK),
+            )
+
+        def quantize_w(g):
+            nc.vector.quantize_mx(
+                out=w_codes[g][:].bitcast(FP8X4),
+                scales=w_scales[g][:],
+                in_=w_bf[g][:].rearrange("p t m j -> p (t m j)"),
+            )
+
+        x_codes = [keep.tile([P, S], U32, name=f"x_codes{g}", align_bytes=64) for g in range(PASSES)]
+        x_bytes = keep.tile([P, S], U8, name="x_bytes", align_bytes=64)
+
+        nc.vector.tensor_copy(x_codes[0][:], x0[:].indirect(offsets[:]))
+        nc.vector.tensor_copy(x_bytes[:], scale_table[:].indirect(offsets[:]))
+        cast_w(nc.scalar.copy, 0, w0a, 0, 0, 64)
+        cast_w(nc.scalar.copy, 0, w0b, 64, 64, 128)
+        quantize_w(0)
+        cast_w(nc.scalar.copy, 1, w1a, 0, 0, 44)
+        cast_w(nc.vector.tensor_copy, 1, w1a, 0, 44, 96)
+        cast_w(nc.vector.tensor_copy, 1, w1b, 96, 96, 128)
+        quantize_w(1)
+        for a, b in FIRST_SLICES:
+            nc.vector.tensor_copy(x_codes[1][:, a:b], x1[:].indirect(picks(a, b)))
+
+        units = [(0, a, b) for a, b in FIRST_SLICES] + [(t, 0, S) for t in range(1, PACK)]
+        banks = [psum.tile([P, b - a], F32, name=f"acc{t}_{a}") for t, a, b in units]
+        for (t, a, b), acc in zip(units, banks):
+            for g in range(PASSES):
+                nc.tensor.matmul_mx(
+                    out=acc[:],
+                    lhsT=w_codes[g][:, t * P : (t + 1) * P].bitcast(FP8X4),
+                    lhsT_scale=w_scales[g][:, t * P : (t + 1) * P],
+                    rhs=x_codes[g][:, a:b].bitcast(FP8X4),
+                    rhs_scale=x_bytes[4 * g : P, a:b],
+                    start=(g == 0),
+                    stop=(g == PASSES - 1),
+                )
+
+        grouped = [keep.tile([P, b - a, PACK], BF16, name=f"grouped{a}", align_bytes=64) for a, b in OUT_CHUNKS]
+        ys = []
+        for (t, a, b), acc in zip(units, banks):
+            y = keep.tile([P, b - a], F32, name=f"y{t}_{a}", align_bytes=64)
+            nc.scalar.activation(y[:], acc[:], GELU)
+            ys.append(y)
+        for (t, a, b), y in zip(units, ys):
+            nc.vector.tensor_copy(windows[t][:].indirect(picks(a, b)), y[:])
+            if b == S:
+                nc.sync.dma_start(out_rows[:, t, :], windows[t][:])
+                for c, (c0, c1) in enumerate(OUT_CHUNKS):
+                    src = windows[t][:, c0:c1]
+                    if c == 0 and t == PACK - 1:
+                        nc.vector.tensor_copy(grouped[c][:, :, t], src)
+                    elif c == 0 and t == PACK - 2:
+                        nc.scalar.copy(grouped[c][:, :, t:], src.unsqueeze(2).to_broadcast([P, c1 - c0, 2]))
+                    else:
+                        nc.scalar.copy(grouped[c][:, :, t], src)
+
+        out_codes = keep.tile([P, T], U32, name="out_codes", align_bytes=64)
+        out_scales = keep.tile([P, T], U8, name="out_scales", align_bytes=64)
+        words = out_1[0].rearrange("p n t -> p (n t)").bitcast(I32)
+        for c, (c0, c1) in enumerate(OUT_CHUNKS):
+            nc.vector.quantize_mx(
+                out=out_codes[:, c0:c1].bitcast(FP8X4),
+                scales=out_scales[:, c0:c1],
+                in_=grouped[c][:].rearrange("p c t -> p (c t)"),
+            )
+            nc.sync.dma_start(words[:, c0:c1], out_codes[:, c0:c1].bitcast(I32))
+        for q in range(4):
+            queue = nc.sync if q % 2 == 0 else nc.scalar
+            queue.dma_start(
+                out_2[0, 4 * q : 4 * q + 4, :].bitcast(I32),
+                out_scales[32 * q : 32 * q + 4, :].bitcast(I32),
+            )

@@ -19,7 +19,7 @@ PACK = 4
 K_PASS = P * PACK
 PASSES = K // K_PASS
 LIST_ROWS = 16
-FIRST_SLICES = ((0, 128), (128, 256), (256, 512))
+FIRST_SLICES = ((0, 128), (128, 512))
 OUT_CHUNKS = ((0, 512), (512, 768), (768, 1024))
 
 
@@ -38,33 +38,35 @@ def tile_picked_zmae_lingelu_po_kernel(
             return offsets[:, a // LIST_ROWS : b // LIST_ROWS]
 
         scale_table = keep.tile([P, T], U8, name="scale_table", align_bytes=64)
-        nc.gpsimd.memset(scale_table[:].bitcast(I32), 0)
+        nc.vector.memset(scale_table[:].bitcast(I32), 0)
+        scale_rows = keep.tile([P, T], U8, name="scale_rows", align_bytes=64)
 
-        def load_w(g, a, b):
+        warm = keep.tile([P, 16], F32, name="warm", align_bytes=64)
+        nc.vector.memset(warm[:, 0:8], 0.0)
+        nc.scalar.activation(warm[:, 8:16], warm[:, 0:8], GELU)
+
+        def load_w(g, a, b, queue=nc.sync):
             raw = keep.tile([P, PACK, b - a], F32, name=f"w_raw{g}_{a}", align_bytes=64)
             rows = w1[g * K_PASS : (g + 1) * K_PASS, a:b]
-            nc.sync.dma_start(raw[:], rows.rearrange("(p j) c -> p j c", j=PACK))
+            queue.dma_start(raw[:], rows.rearrange("(p j) c -> p j c", j=PACK))
             return raw
 
-        def load_x(g, pieces):
+        def load_x(g, queue):
             table = keep.tile([P, T], U32, name=f"word_table{g}", align_bytes=64)
             words_in = x_words[g].rearrange("p n t -> p (n t)").bitcast(I32)
-            width = T // pieces
-            for a in range(0, T, width):
-                nc.sync.dma_start(table[:, a : a + width].bitcast(I32), words_in[:, a : a + width])
+            queue.dma_start(table[:].bitcast(I32), words_in)
             return table
 
         for q in range(4):
-            nc.sync.dma_start(
-                scale_table[32 * q : 32 * q + 4 * PASSES, :].bitcast(I32),
-                x_scales[:, 4 * q : 4 * q + 4, :].bitcast(I32),
-            )
-        x0 = load_x(0, 2)
-        w0a = load_w(0, 0, M // 2)
+            live = slice(32 * q, 32 * q + 4 * PASSES)
+            nc.sync.dma_start(scale_rows[live, :].bitcast(I32), x_scales[:, 4 * q : 4 * q + 4, :].bitcast(I32))
+            nc.vector.tensor_copy(scale_table[live, :].bitcast(I32), scale_rows[live, :].bitcast(I32))
+        w0a = load_w(0, 0, M // 2, nc.scalar)
         w0b = load_w(0, M // 2, M)
-        w1a = load_w(1, 0, 384)
-        w1b = load_w(1, 384, M)
-        x1 = load_x(1, 1)
+        w1a = load_w(1, 0, M // 2)
+        w1b = load_w(1, M // 2, M)
+        x0 = load_x(0, nc.sync)
+        x1 = load_x(1, nc.sync)
         mask_rows = mask.rearrange("(p t) c -> p t c", t=PACK)
         out_rows = out_0.rearrange("(p t) c -> p t c", t=PACK)
         windows = []
@@ -73,7 +75,9 @@ def tile_picked_zmae_lingelu_po_kernel(
             nc.sync.dma_start(window[:], mask_rows[:, t, :])
             windows.append(window)
 
-        w_bf = [keep.tile([P, PACK, P, PACK], BF16, name=f"w_bf{g}", align_bytes=64) for g in range(PASSES)]
+        w_tiles = [keep.tile([P, M * PACK], BF16, name=f"w_bf{g}", align_bytes=64) for g in range(PASSES)]
+        w_flat = [tile[:] for tile in w_tiles]
+        w_bf = [flat.rearrange("p (t m j) -> p t m j", t=PACK, j=PACK) for flat in w_flat]
         w_codes = [keep.tile([P, M], U32, name=f"w_codes{g}", align_bytes=64) for g in range(PASSES)]
         w_scales = [keep.tile([P, M], U8, name=f"w_scales{g}", align_bytes=64) for g in range(PASSES)]
 
@@ -87,27 +91,26 @@ def tile_picked_zmae_lingelu_po_kernel(
             nc.vector.quantize_mx(
                 out=w_codes[g][:].bitcast(FP8X4),
                 scales=w_scales[g][:],
-                in_=w_bf[g][:].rearrange("p t m j -> p (t m j)"),
+                in_=w_flat[g],
             )
 
-        x_codes = [keep.tile([P, S], U32, name=f"x_codes{g}", align_bytes=64) for g in range(PASSES)]
         x_bytes = keep.tile([P, S], U8, name="x_bytes", align_bytes=64)
 
-        nc.vector.tensor_copy(x_codes[0][:], x0[:].indirect(offsets[:]))
         nc.vector.tensor_copy(x_bytes[:], scale_table[:].indirect(offsets[:]))
         cast_w(nc.scalar.copy, 0, w0a, 0, 0, 64)
-        cast_w(nc.scalar.copy, 0, w0b, 64, 64, 128)
+        cast_w(nc.vector.tensor_copy, 0, w0b, 64, 64, 128)
         quantize_w(0)
-        cast_w(nc.scalar.copy, 1, w1a, 0, 0, 44)
-        cast_w(nc.vector.tensor_copy, 1, w1a, 0, 44, 96)
-        cast_w(nc.vector.tensor_copy, 1, w1b, 96, 96, 128)
+        cast_w(nc.scalar.copy, 1, w1a, 0, 0, 64)
+        cast_w(nc.vector.tensor_copy, 1, w1b, 64, 64, 128)
         quantize_w(1)
+        picked = keep.tile([P, PASSES * S], U32, name="picked", tag="w_bf1", align_bytes=64)
+        x_codes = [picked[:, g * S : (g + 1) * S] for g in range(PASSES)]
+        nc.vector.tensor_copy(x_codes[0], x0[:].indirect(offsets[:]))
         for a, b in FIRST_SLICES:
             nc.vector.tensor_copy(x_codes[1][:, a:b], x1[:].indirect(picks(a, b)))
 
-        units = [(0, a, b) for a, b in FIRST_SLICES] + [(t, 0, S) for t in range(1, PACK)]
-        banks = [psum.tile([P, b - a], F32, name=f"acc{t}_{a}") for t, a, b in units]
-        for (t, a, b), acc in zip(units, banks):
+        def product(t, a, b, y, tag):
+            acc = psum.tile([P, b - a], F32, name=f"acc{t}_{a}", tag=tag)
             for g in range(PASSES):
                 nc.tensor.matmul_mx(
                     out=acc[:],
@@ -118,13 +121,18 @@ def tile_picked_zmae_lingelu_po_kernel(
                     start=(g == 0),
                     stop=(g == PASSES - 1),
                 )
+            nc.scalar.activation(y, acc[:], GELU)
+
+        units = [(0, a, b) for a, b in FIRST_SLICES] + [(t, 0, S) for t in range(1, PACK)]
+        ys = [keep.tile([P, b - a], F32, name=f"y{t}_{a}", align_bytes=64) for t, a, b in units]
+        product(0, 0, 128, ys[0][:], "bank0")
+        product(0, 128, 256, ys[1][:, :128], "bank1")
+        product(0, 256, S, ys[1][:, 128:], "bank2")
+        product(1, 0, S, ys[2][:], "bank0")
+        product(2, 0, S, ys[3][:], "bank1")
+        product(3, 0, S, ys[4][:], "bank2")
 
         grouped = [keep.tile([P, b - a, PACK], BF16, name=f"grouped{a}", align_bytes=64) for a, b in OUT_CHUNKS]
-        ys = []
-        for (t, a, b), acc in zip(units, banks):
-            y = keep.tile([P, b - a], F32, name=f"y{t}_{a}", align_bytes=64)
-            nc.scalar.activation(y[:], acc[:], GELU)
-            ys.append(y)
         for (t, a, b), y in zip(units, ys):
             nc.vector.tensor_copy(windows[t][:].indirect(picks(a, b)), y[:])
             if b == S:

@@ -45,9 +45,9 @@ def tile_picked_zmae_lingelu_po_kernel(
         nc.vector.memset(warm[:, 0:8], 0.0)
         nc.scalar.activation(warm[:, 8:16], warm[:, 0:8], GELU)
 
-        def load_w(g, a, b, queue=nc.sync):
-            raw = keep.tile([P, PACK, b - a], F32, name=f"w_raw{g}_{a}", align_bytes=64)
-            rows = w1[g * K_PASS : (g + 1) * K_PASS, a:b]
+        def load_w(g, queue):
+            raw = keep.tile([P, PACK, M], F32, name=f"w_raw{g}", align_bytes=64)
+            rows = w1[g * K_PASS : (g + 1) * K_PASS, :]
             queue.dma_start(raw[:], rows.rearrange("(p j) c -> p j c", j=PACK))
             return raw
 
@@ -61,11 +61,8 @@ def tile_picked_zmae_lingelu_po_kernel(
             live = slice(32 * q, 32 * q + 4 * PASSES)
             nc.sync.dma_start(scale_rows[live, :].bitcast(I32), x_scales[:, 4 * q : 4 * q + 4, :].bitcast(I32))
             nc.vector.tensor_copy(scale_table[live, :].bitcast(I32), scale_rows[live, :].bitcast(I32))
-        w0a = load_w(0, 0, M // 2, nc.scalar)
-        w0b = load_w(0, M // 2, M)
-        w1a = load_w(1, 0, M // 2)
-        w1b = load_w(1, M // 2, M)
-        x0 = load_x(0, nc.sync)
+        x0 = load_x(0, nc.scalar)
+        w_raw = [load_w(0, nc.sync), load_w(1, nc.sync)]
         x1 = load_x(1, nc.sync)
         mask_rows = mask.rearrange("(p t) c -> p t c", t=PACK)
         out_rows = out_0.rearrange("(p t) c -> p t c", t=PACK)
@@ -75,39 +72,33 @@ def tile_picked_zmae_lingelu_po_kernel(
             nc.sync.dma_start(window[:], mask_rows[:, t, :])
             windows.append(window)
 
-        w_tiles = [keep.tile([P, M * PACK], BF16, name=f"w_bf{g}", align_bytes=64) for g in range(PASSES)]
-        w_flat = [tile[:] for tile in w_tiles]
-        w_bf = [flat.rearrange("p (t m j) -> p t m j", t=PACK, j=PACK) for flat in w_flat]
         w_codes = [keep.tile([P, M], U32, name=f"w_codes{g}", align_bytes=64) for g in range(PASSES)]
         w_scales = [keep.tile([P, M], U8, name=f"w_scales{g}", align_bytes=64) for g in range(PASSES)]
 
-        def cast_w(copy, g, raw, raw0, a, b):
+        def cast_w(copy, g, h):
+            rounded = keep.tile([P, 2 * P * PACK], BF16, name=f"w_bf{g}_{h}", tag=f"w_bf{g}_{h}" if h else "lead", align_bytes=64)
             copy(
-                w_bf[g][:, :, a:b, :].rearrange("p t m j -> p m j t"),
-                raw[:, :, PACK * (a - raw0) : PACK * (b - raw0)].rearrange("p j (m t) -> p m j t", t=PACK),
+                rounded[:].rearrange("p (t m j) -> p m j t", m=P, j=PACK),
+                w_raw[g][:].rearrange("p j (m t) -> p m j t", t=PACK)[:, :, :, 2 * h : 2 * h + 2],
             )
+            return rounded
 
-        def quantize_w(g):
-            nc.vector.quantize_mx(
-                out=w_codes[g][:].bitcast(FP8X4),
-                scales=w_scales[g][:],
-                in_=w_flat[g],
-            )
+        def quantize_w(g, h, rounded):
+            cols = slice(2 * h * P, 2 * (h + 1) * P)
+            nc.vector.quantize_mx(out=w_codes[g][:, cols].bitcast(FP8X4), scales=w_scales[g][:, cols], in_=rounded[:])
 
         x_bytes = keep.tile([P, S], U8, name="x_bytes", align_bytes=64)
-
         nc.vector.tensor_copy(x_bytes[:], scale_table[:].indirect(offsets[:]))
-        cast_w(nc.scalar.copy, 0, w0a, 0, 0, 64)
-        cast_w(nc.vector.tensor_copy, 0, w0b, 64, 64, 128)
-        quantize_w(0)
-        cast_w(nc.scalar.copy, 1, w1a, 0, 0, 64)
-        cast_w(nc.vector.tensor_copy, 1, w1b, 64, 64, 128)
-        quantize_w(1)
-        picked = keep.tile([P, PASSES * S], U32, name="picked", tag="w_bf1", align_bytes=64)
-        x_codes = [picked[:, g * S : (g + 1) * S] for g in range(PASSES)]
-        nc.vector.tensor_copy(x_codes[0], x0[:].indirect(offsets[:]))
+        x_codes = [keep.tile([P, S], U32, name="x_codes0", align_bytes=64)]
+        nc.vector.tensor_copy(x_codes[0][:], x0[:].indirect(offsets[:]))
+        quantize_w(0, 0, cast_w(nc.scalar.copy, 0, 0))
+        quantize_w(0, 1, cast_w(nc.scalar.copy, 0, 1))
+        quantize_w(1, 0, cast_w(nc.vector.tensor_copy, 1, 0))
+        late = cast_w(nc.scalar.copy, 1, 1)
+        x_codes.append(keep.tile([P, S], U32, name="x_codes1", tag="lead", align_bytes=64))
         for a, b in FIRST_SLICES:
             nc.vector.tensor_copy(x_codes[1][:, a:b], x1[:].indirect(picks(a, b)))
+        quantize_w(1, 1, late)
 
         def product(t, a, b, y, tag):
             acc = psum.tile([P, b - a], F32, name=f"acc{t}_{a}", tag=tag)

@@ -41,10 +41,6 @@ def tile_picked_zmae_lingelu_po_kernel(
         nc.vector.memset(scale_table[:].bitcast(I32), 0)
         scale_rows = keep.tile([P, T], U8, name="scale_rows", align_bytes=64)
 
-        warm = keep.tile([P, 16], F32, name="warm", align_bytes=64)
-        nc.vector.memset(warm[:, 0:8], 0.0)
-        nc.scalar.activation(warm[:, 8:16], warm[:, 0:8], GELU)
-
         def load_w(g, queue):
             raw = keep.tile([P, PACK, M], F32, name=f"w_raw{g}", align_bytes=64)
             rows = w1[g * K_PASS : (g + 1) * K_PASS, :]
@@ -92,8 +88,9 @@ def tile_picked_zmae_lingelu_po_kernel(
         x_codes = [keep.tile([P, S], U32, name="x_codes0", align_bytes=64)]
         nc.vector.tensor_copy(x_codes[0][:], x0[:].indirect(offsets[:]))
         quantize_w(0, 0, cast_w(nc.scalar.copy, 0, 0))
-        quantize_w(0, 1, cast_w(nc.scalar.copy, 0, 1))
+        early = cast_w(nc.scalar.copy, 0, 1)
         quantize_w(1, 0, cast_w(nc.vector.tensor_copy, 1, 0))
+        quantize_w(0, 1, early)
         late = cast_w(nc.scalar.copy, 1, 1)
         x_codes.append(keep.tile([P, S], U32, name="x_codes1", tag="lead", align_bytes=64))
         for a, b in FIRST_SLICES:
@@ -119,9 +116,9 @@ def tile_picked_zmae_lingelu_po_kernel(
         product(0, 0, 128, ys[0][:], "bank0")
         product(0, 128, 256, ys[1][:, :128], "bank1")
         product(0, 256, S, ys[1][:, 128:], "bank2")
-        product(1, 0, S, ys[2][:], "bank0")
-        product(2, 0, S, ys[3][:], "bank1")
-        product(3, 0, S, ys[4][:], "bank2")
+        product(1, 0, S, ys[2][:], "bank3")
+        product(2, 0, S, ys[3][:], "bank4")
+        product(3, 0, S, ys[4][:], "bank5")
 
         grouped = [keep.tile([P, b - a, PACK], BF16, name=f"grouped{a}", align_bytes=64) for a, b in OUT_CHUNKS]
         for (t, a, b), y in zip(units, ys):

@@ -1,6 +1,7 @@
 from contextlib import ExitStack
 
 import concourse.mybir as mybir
+from concourse.masks import make_identity
 
 K, T, S, M = 1024, 1024, 512, 512
 FLOPS = 2 * K * S * M
@@ -19,8 +20,10 @@ PACK = 4
 K_PASS = P * PACK
 PASSES = K // K_PASS
 LIST_ROWS = 16
-FIRST_SLICES = ((0, 128), (128, 512))
-OUT_CHUNKS = ((0, 512), (512, 768), (768, 1024))
+HALF = P // 2
+LEAD = 128
+CHUNK = 256
+BANK = 512
 
 
 def tile_picked_zmae_lingelu_po_kernel(
@@ -29,6 +32,7 @@ def tile_picked_zmae_lingelu_po_kernel(
     nc = tc.nc
     with ExitStack() as ctx:
         keep = ctx.enter_context(tc.tile_pool(name="keep", bufs=1))
+        stage = ctx.enter_context(tc.tile_pool(name="stage", bufs=1))
         psum = ctx.enter_context(tc.psum_pool(name="psum", bufs=1))
 
         offsets = keep.tile([P, S // LIST_ROWS], U16, name="offsets")
@@ -38,14 +42,14 @@ def tile_picked_zmae_lingelu_po_kernel(
             return offsets[:, a // LIST_ROWS : b // LIST_ROWS]
 
         scale_table = keep.tile([P, T], U8, name="scale_table", align_bytes=64)
-        nc.vector.memset(scale_table[:].bitcast(I32), 0)
-        scale_rows = keep.tile([P, T], U8, name="scale_rows", align_bytes=64)
+        nc.gpsimd.memset(scale_table[:].bitcast(I32), 0)
 
-        def load_w(g, queue):
-            raw = keep.tile([P, PACK, M], F32, name=f"w_raw{g}", align_bytes=64)
-            rows = w1[g * K_PASS : (g + 1) * K_PASS, :]
-            queue.dma_start(raw[:], rows.rearrange("(p j) c -> p j c", j=PACK))
-            return raw
+        def load_w(h, g):
+            tag = "last_rows" if (h, g) == (1, PASSES - 1) else f"w_raw{h}_{g}"
+            raw = keep.tile([P, PACK, M // 2], F32, name=f"w_raw{h}_{g}", tag=tag, align_bytes=64)
+            rows = w1[g * K_PASS : (g + 1) * K_PASS, h * M // 2 : (h + 1) * M // 2]
+            nc.sync.dma_start(raw[:], rows.rearrange("(p j) c -> p j c", j=PACK))
+            return raw[:].rearrange("p j (i t) -> p i j t", t=PACK)
 
         def load_x(g, queue):
             table = keep.tile([P, T], U32, name=f"word_table{g}", align_bytes=64)
@@ -53,97 +57,171 @@ def tile_picked_zmae_lingelu_po_kernel(
             queue.dma_start(table[:].bitcast(I32), words_in)
             return table
 
+        def rows_of(dram, u):
+            dealt = dram.rearrange("(p t) c -> p t c", t=PACK)
+            return dealt[u * HALF : (u + 1) * HALF, 0:2, :] if u < 2 else dealt[:, u, :]
+
+        def load_window(u):
+            window = keep.tile([P, T], F32, name=f"window{u}", align_bytes=64)
+            nc.sync.dma_start(window[:], rows_of(mask, u))
+            return window
+
         for q in range(4):
             live = slice(32 * q, 32 * q + 4 * PASSES)
-            nc.sync.dma_start(scale_rows[live, :].bitcast(I32), x_scales[:, 4 * q : 4 * q + 4, :].bitcast(I32))
-            nc.vector.tensor_copy(scale_table[live, :].bitcast(I32), scale_rows[live, :].bitcast(I32))
+            nc.sync.dma_start(scale_table[live, :].bitcast(I32), x_scales[:, 4 * q : 4 * q + 4, :].bitcast(I32))
         x0 = load_x(0, nc.scalar)
-        w_raw = [load_w(0, nc.sync), load_w(1, nc.sync)]
+        w_raw = {(0, g): load_w(0, g) for g in range(PASSES)}
         x1 = load_x(1, nc.sync)
-        mask_rows = mask.rearrange("(p t) c -> p t c", t=PACK)
-        out_rows = out_0.rearrange("(p t) c -> p t c", t=PACK)
-        windows = []
-        for t in range(PACK):
-            window = keep.tile([P, T], F32, name=f"window{t}", align_bytes=64)
-            nc.sync.dma_start(window[:], mask_rows[:, t, :])
-            windows.append(window)
+        windows = [load_window(0)]
+        for g in range(PASSES):
+            w_raw[1, g] = load_w(1, g)
+        windows.extend(load_window(u) for u in range(1, PACK))
 
-        w_codes = [keep.tile([P, M], U32, name=f"w_codes{g}", align_bytes=64) for g in range(PASSES)]
-        w_scales = [keep.tile([P, M], U8, name=f"w_scales{g}", align_bytes=64) for g in range(PASSES)]
+        warm_in = keep.tile([P, 1], F32, name="warm_in")
+        warm_out = keep.tile([P, 1], F32, name="warm_out")
+        nc.vector.memset(warm_in[:], 0.0)
+        nc.scalar.activation(warm_out[:], warm_in[:], GELU)
+        identity = keep.tile([P, P], F32, name="identity", align_bytes=64)
+        make_identity(nc, identity[:])
 
-        def cast_w(copy, g, h):
-            rounded = keep.tile([P, 2 * P * PACK], BF16, name=f"w_bf{g}_{h}", tag=f"w_bf{g}_{h}" if h else "lead", align_bytes=64)
-            copy(
-                rounded[:].rearrange("p (t m j) -> p m j t", m=P, j=PACK),
-                w_raw[g][:].rearrange("p j (m t) -> p m j t", t=PACK)[:, :, :, 2 * h : 2 * h + 2],
-            )
-            return rounded
+        lead_bf = [keep.tile([P, PASSES * K_PASS], BF16, name=f"lead_bf{h}", align_bytes=64) for h in range(2)]
+        late_bf = keep.tile([P, 2 * PASSES * K_PASS], BF16, name="late_bf", align_bytes=64)
 
-        def quantize_w(g, h, rounded):
-            cols = slice(2 * h * P, 2 * (h + 1) * P)
-            nc.vector.quantize_mx(out=w_codes[g][:, cols].bitcast(FP8X4), scales=w_scales[g][:, cols], in_=rounded[:])
+        def cast_lead(copy, h, g):
+            dst = lead_bf[h][:].rearrange("p (g i u j) -> p g i j u", g=PASSES, u=2, j=PACK)
+            copy(dst[:, g], w_raw[h, g][:, :, :, 0:2])
 
+        def cast_late(h, g):
+            dst = late_bf[:].rearrange("p (g t h i j) -> p g h i j t", g=PASSES, t=2, h=2, j=PACK)
+            nc.scalar.copy(dst[:, g, h], w_raw[h, g][:, :, :, 2:4])
+
+        def quantize_w(name, rounded):
+            width = rounded.shape[1] // PACK
+            codes = keep.tile([P, width], U32, name=f"{name}_codes", align_bytes=64)
+            scales = keep.tile([P, width], U8, name=f"{name}_scales", align_bytes=64)
+            nc.vector.quantize_mx(out=codes[:].bitcast(FP8X4), scales=scales[:], in_=rounded[:])
+            return codes, scales
+
+        x_codes = [keep.tile([P, S], U32, name=f"x_codes{g}", align_bytes=64) for g in range(PASSES)]
         x_bytes = keep.tile([P, S], U8, name="x_bytes", align_bytes=64)
-        nc.vector.tensor_copy(x_bytes[:], scale_table[:].indirect(offsets[:]))
-        x_codes = [keep.tile([P, S], U32, name="x_codes0", align_bytes=64)]
-        nc.vector.tensor_copy(x_codes[0][:], x0[:].indirect(offsets[:]))
-        quantize_w(0, 0, cast_w(nc.scalar.copy, 0, 0))
-        early = cast_w(nc.scalar.copy, 0, 1)
-        quantize_w(1, 0, cast_w(nc.vector.tensor_copy, 1, 0))
-        quantize_w(0, 1, early)
-        late = cast_w(nc.scalar.copy, 1, 1)
-        x_codes.append(keep.tile([P, S], U32, name="x_codes1", tag="lead", align_bytes=64))
-        for a, b in FIRST_SLICES:
-            nc.vector.tensor_copy(x_codes[1][:, a:b], x1[:].indirect(picks(a, b)))
-        quantize_w(1, 1, late)
+        slices = ((0, LEAD), (LEAD, 2 * LEAD), (2 * LEAD, S))
+        ys = [keep.tile([P, S], F32, name=f"y{u}", align_bytes=64) for u in range(PACK)]
 
-        def product(t, a, b, y, tag):
-            acc = psum.tile([P, b - a], F32, name=f"acc{t}_{a}", tag=tag)
+        def bank(n, name, shape):
+            return psum.tile(shape, F32, name=name, tag=f"bank{n}")
+
+        def product(u, a, b, weights, col, n, y=None):
+            codes, scales = weights
+            stride = codes.shape[1] // PASSES
+            acc = bank(n, f"acc{u}_{a}", [P, b - a])
             for g in range(PASSES):
+                cols = slice(g * stride + col, g * stride + col + P)
                 nc.tensor.matmul_mx(
                     out=acc[:],
-                    lhsT=w_codes[g][:, t * P : (t + 1) * P].bitcast(FP8X4),
-                    lhsT_scale=w_scales[g][:, t * P : (t + 1) * P],
+                    lhsT=codes[:, cols].bitcast(FP8X4),
+                    lhsT_scale=scales[:, cols],
                     rhs=x_codes[g][:, a:b].bitcast(FP8X4),
                     rhs_scale=x_bytes[4 * g : P, a:b],
                     start=(g == 0),
                     stop=(g == PASSES - 1),
                 )
-            nc.scalar.activation(y, acc[:], GELU)
+            nc.scalar.activation(ys[u][:, a:b] if y is None else y, acc[:], GELU)
 
-        units = [(0, a, b) for a, b in FIRST_SLICES] + [(t, 0, S) for t in range(1, PACK)]
-        ys = [keep.tile([P, b - a], F32, name=f"y{t}_{a}", align_bytes=64) for t, a, b in units]
-        product(0, 0, 128, ys[0][:], "bank0")
-        product(0, 128, 256, ys[1][:, :128], "bank1")
-        product(0, 256, S, ys[1][:, 128:], "bank2")
-        product(1, 0, S, ys[2][:], "bank3")
-        product(2, 0, S, ys[3][:], "bank4")
-        product(3, 0, S, ys[4][:], "bank5")
-
-        grouped = [keep.tile([P, b - a, PACK], BF16, name=f"grouped{a}", align_bytes=64) for a, b in OUT_CHUNKS]
-        for (t, a, b), y in zip(units, ys):
-            nc.vector.tensor_copy(windows[t][:].indirect(picks(a, b)), y[:])
+        def scatter(u, a, b, y=None):
+            nc.vector.tensor_copy(windows[u][:].indirect(picks(a, b)), ys[u][:, a:b] if y is None else y)
             if b == S:
-                nc.sync.dma_start(out_rows[:, t, :], windows[t][:])
-                for c, (c0, c1) in enumerate(OUT_CHUNKS):
-                    src = windows[t][:, c0:c1]
-                    if c == 0 and t == PACK - 1:
-                        nc.vector.tensor_copy(grouped[c][:, :, t], src)
-                    elif c == 0 and t == PACK - 2:
-                        nc.scalar.copy(grouped[c][:, :, t:], src.unsqueeze(2).to_broadcast([P, c1 - c0, 2]))
-                    else:
-                        nc.scalar.copy(grouped[c][:, :, t], src)
+                nc.sync.dma_start(rows_of(out_0, u), windows[u][:])
+
+        nc.vector.tensor_copy(x_codes[0][:], x0[:].indirect(offsets[:]))
+        nc.vector.tensor_copy(x_bytes[:], scale_table[:].indirect(offsets[:]))
+        cast_lead(nc.scalar.copy, 0, 0)
+        cast_lead(nc.vector.tensor_copy, 0, 1)
+        lead0 = quantize_w("lead0", lead_bf[0])
+        cast_late(0, 0)
+        cast_late(0, 1)
+        for a, b in ((0, LEAD), (LEAD, S - LEAD), (S - LEAD, S)):
+            nc.vector.tensor_copy(x_codes[1][:, a:b], x1[:].indirect(picks(a, b)))
+        product(0, 0, LEAD, lead0, 0, 0)
+        product(0, LEAD, S - LEAD, lead0, 0, 1)
+        scatter(0, 0, LEAD)
+        scatter(0, LEAD, S - LEAD)
+
+        for g in range(PASSES):
+            cast_lead(nc.scalar.copy, 1, g)
+        lead1 = quantize_w("lead1", lead_bf[1])
+        for g in range(PASSES):
+            cast_late(1, g)
+        late = quantize_w("late", late_bf)
+        y_rest = keep.tile([P, LEAD], F32, name="y_rest", tag="last_rows", align_bytes=64)
+        product(0, S - LEAD, S, lead0, 0, 2, y_rest[:])
+        scatter(0, S - LEAD, S, y_rest[:])
+        for n, (a, b) in enumerate(slices):
+            product(1, a, b, lead1, 0, 3 + n)
+        product(2, 0, S, late, 0, 6)
+        product(3, 0, S, late, P, 7)
+        scatter(1, 0, LEAD)
+        scatter(1, LEAD, S)
+        scatter(2, 0, S)
+        scatter(3, 0, S)
+
+        blocks = BANK // P
+        turned = [
+            stage.tile([P, blocks, 2 * P], BF16, name=f"turned{k}", align_bytes=64, offset=4096 * k + 1024)
+            for k in range(2)
+        ]
+        for u, first_bank in ((0, 3), (1, 6)):
+            for k in range(2):
+                across = bank(first_bank + k, f"across{u}_{k}", [P, blocks, P])
+                for b in range(blocks):
+                    c0 = k * BANK + b * P
+                    nc.tensor.transpose(across[:, b, :], windows[u][:, c0 : c0 + P], identity[:])
+                nc.scalar.copy(turned[k][:, :, u * P : (u + 1) * P], across[:])
+
+        backs = []
+        for k in range(2):
+            back = bank(k, f"back{k}", [P, blocks, P])
+            for b in range(blocks):
+                nc.tensor.transpose(back[:, b, :], turned[k][:, b, :].bitcast(F32), identity[:])
+            backs.append(back[:].rearrange("p b c -> p (b c)"))
+        pairs = stage.tile([P, 2, 2 * T], BF16, name="pairs", align_bytes=64, offset=0)
+        for k in range(2):
+            nc.scalar.copy(pairs[:, 0, 2 * k * BANK : 2 * (k + 1) * BANK].bitcast(F32), backs[k])
+        uppers = pairs[:, 1, :].rearrange("p (c e) -> p c e", e=2)
+        nc.scalar.copy(uppers, windows[2][:].unsqueeze(2).to_broadcast([P, T, 2]))
+
+        def upper(c):
+            return uppers[:, c * CHUNK : (c + 1) * CHUNK, :]
+
+        def cols(u, c):
+            return windows[u][:, c * CHUNK : (c + 1) * CHUNK]
 
         out_codes = keep.tile([P, T], U32, name="out_codes", align_bytes=64)
         out_scales = keep.tile([P, T], U8, name="out_scales", align_bytes=64)
         words = out_1[0].rearrange("p n t -> p (n t)").bitcast(I32)
-        for c, (c0, c1) in enumerate(OUT_CHUNKS):
-            nc.vector.quantize_mx(
-                out=out_codes[:, c0:c1].bitcast(FP8X4),
-                scales=out_scales[:, c0:c1],
-                in_=grouped[c][:].rearrange("p c t -> p (c t)"),
+        woven = [keep.tile([P, CHUNK * PACK], BF16, name=f"woven{c}", align_bytes=64) for c in range(T // CHUNK)]
+
+        def weave(copy, dtype, c):
+            copy(
+                woven[c][:].bitcast(dtype).rearrange("p (c u) -> p c u", u=2),
+                pairs[:].bitcast(dtype)[:, :, c * CHUNK : (c + 1) * CHUNK].rearrange("p u c -> p c u"),
             )
-            nc.sync.dma_start(words[:, c0:c1], out_codes[:, c0:c1].bitcast(I32))
+
+        nc.scalar.copy(upper(2)[:, :, 1], cols(3, 2))
+        for c in (3, 0, 1):
+            nc.vector.tensor_copy(upper(c)[:, :, 1], cols(3, c))
+        for c in (2, 3):
+            weave(nc.scalar.copy, U32, c)
+        for c in (0, 1):
+            weave(nc.vector.tensor_copy, I32, c)
+        codes_by_chunk = out_codes[:].bitcast(I32).rearrange("p (a b c) -> p a b c", a=2, b=2)
+        words_by_chunk = words.rearrange("p (a b c) -> p a b c", a=2, b=2)
+        for c in (0, 2, 1, 3):
+            at = slice(c * CHUNK, (c + 1) * CHUNK)
+            nc.vector.quantize_mx(out=out_codes[:, at].bitcast(FP8X4), scales=out_scales[:, at], in_=woven[c][:])
+            if c == 2:
+                nc.sync.dma_start(words_by_chunk[:, :, 0, :], codes_by_chunk[:, :, 0, :])
+            elif c > 0:
+                nc.sync.dma_start(words[:, at], out_codes[:, at].bitcast(I32))
         for q in range(4):
             queue = nc.sync if q % 2 == 0 else nc.scalar
             queue.dma_start(

@@ -66,11 +66,12 @@ def tile_picked_zmae_lingelu_po_kernel(
             nc.sync.dma_start(window[:], rows_of(mask, u))
             return window
 
+        x0 = load_x(0, nc.scalar)
+        w_raw = {(0, 0): load_w(0, 0)}
         for q in range(4):
             live = slice(32 * q, 32 * q + 4 * PASSES)
             nc.sync.dma_start(scale_table[live, :].bitcast(I32), x_scales[:, 4 * q : 4 * q + 4, :].bitcast(I32))
-        x0 = load_x(0, nc.scalar)
-        w_raw = {(0, g): load_w(0, g) for g in range(PASSES)}
+        w_raw[0, 1] = load_w(0, 1)
         x1 = load_x(1, nc.sync)
         windows = [load_window(0)]
         for g in range(PASSES):
@@ -170,27 +171,31 @@ def tile_picked_zmae_lingelu_po_kernel(
             for k in range(2)
         ]
         for u, first_bank in ((0, 3), (1, 6)):
-            for k in range(2):
+            for k in (1, 0):
                 across = bank(first_bank + k, f"across{u}_{k}", [P, blocks, P])
                 for b in range(blocks):
                     c0 = k * BANK + b * P
                     nc.tensor.transpose(across[:, b, :], windows[u][:, c0 : c0 + P], identity[:])
                 nc.scalar.copy(turned[k][:, :, u * P : (u + 1) * P], across[:])
 
-        backs = []
-        for k in range(2):
+        pairs = {}
+        for k in (1, 0):
             back = bank(k, f"back{k}", [P, blocks, P])
             for b in range(blocks):
                 nc.tensor.transpose(back[:, b, :], turned[k][:, b, :].bitcast(F32), identity[:])
-            backs.append(back[:].rearrange("p b c -> p (b c)"))
-        pairs = stage.tile([P, 2, 2 * T], BF16, name="pairs", align_bytes=64, offset=0)
-        for k in range(2):
-            nc.scalar.copy(pairs[:, 0, 2 * k * BANK : 2 * (k + 1) * BANK].bitcast(F32), backs[k])
-        uppers = pairs[:, 1, :].rearrange("p (c e) -> p c e", e=2)
-        nc.scalar.copy(uppers, windows[2][:].unsqueeze(2).to_broadcast([P, T, 2]))
+            pairs[k] = stage.tile([P, 2, 2 * BANK], BF16, name=f"pairs{k}", align_bytes=64, offset=4096 * k)
+            nc.scalar.copy(pairs[k][:, 0, :].bitcast(F32), back[:].rearrange("p b c -> p (b c)"))
+        for k in (1, 0):
+            plane = windows[2][:, k * BANK : (k + 1) * BANK].rearrange("p (h c) -> p h c", h=2)
+            uppers = pairs[k][:, 1, :].rearrange("p (h c e) -> p h c e", h=2, e=2)
+            nc.scalar.copy(uppers[:, :, 1:, 0], plane[:, :, 1:])
+            nc.scalar.copy(uppers[:, :, 0, :], plane[:, :, 0:1].to_broadcast([P, 2, 2]))
+
+        def within(c):
+            return slice((c % 2) * CHUNK, (c % 2 + 1) * CHUNK)
 
         def upper(c):
-            return uppers[:, c * CHUNK : (c + 1) * CHUNK, :]
+            return pairs[c // 2][:, 1, :].rearrange("p (c e) -> p c e", e=2)[:, within(c), :]
 
         def cols(u, c):
             return windows[u][:, c * CHUNK : (c + 1) * CHUNK]
@@ -200,28 +205,31 @@ def tile_picked_zmae_lingelu_po_kernel(
         words = out_1[0].rearrange("p n t -> p (n t)").bitcast(I32)
         woven = [keep.tile([P, CHUNK * PACK], BF16, name=f"woven{c}", align_bytes=64) for c in range(T // CHUNK)]
 
-        def weave(copy, dtype, c):
+        def weave(copy, c):
             copy(
-                woven[c][:].bitcast(dtype).rearrange("p (c u) -> p c u", u=2),
-                pairs[:].bitcast(dtype)[:, :, c * CHUNK : (c + 1) * CHUNK].rearrange("p u c -> p c u"),
+                woven[c][:].rearrange("p (c u e) -> p c u e", u=2, e=2),
+                pairs[c // 2][:].rearrange("p u (c e) -> p c u e", e=2)[:, within(c)],
+            )
+
+        def weave_words(c):
+            nc.scalar.copy(
+                woven[c][:].bitcast(U32).rearrange("p (c u) -> p c u", u=2),
+                pairs[c // 2][:].bitcast(U32)[:, :, within(c)].rearrange("p u c -> p c u"),
             )
 
         nc.scalar.copy(upper(2)[:, :, 1], cols(3, 2))
         for c in (3, 0, 1):
             nc.vector.tensor_copy(upper(c)[:, :, 1], cols(3, c))
         for c in (2, 3):
-            weave(nc.scalar.copy, U32, c)
+            weave_words(c)
         for c in (0, 1):
-            weave(nc.vector.tensor_copy, I32, c)
-        codes_by_chunk = out_codes[:].bitcast(I32).rearrange("p (a b c) -> p a b c", a=2, b=2)
-        words_by_chunk = words.rearrange("p (a b c) -> p a b c", a=2, b=2)
-        for c in (0, 2, 1, 3):
+            weave(nc.vector.tensor_copy, c)
+        for c in range(T // CHUNK):
             at = slice(c * CHUNK, (c + 1) * CHUNK)
             nc.vector.quantize_mx(out=out_codes[:, at].bitcast(FP8X4), scales=out_scales[:, at], in_=woven[c][:])
-            if c == 2:
-                nc.sync.dma_start(words_by_chunk[:, :, 0, :], codes_by_chunk[:, :, 0, :])
-            elif c > 0:
-                nc.sync.dma_start(words[:, at], out_codes[:, at].bitcast(I32))
+            if c > 0:
+                stored = slice(0, 2 * CHUNK) if c == 1 else at
+                nc.sync.dma_start(words[:, stored], out_codes[:, stored].bitcast(I32))
         for q in range(4):
             queue = nc.sync if q % 2 == 0 else nc.scalar
             queue.dma_start(

@@ -78,10 +78,6 @@ def tile_picked_zmae_lingelu_po_kernel(
             w_raw[1, g] = load_w(1, g)
         windows.extend(load_window(u) for u in range(1, PACK))
 
-        warm_in = keep.tile([P, 1], F32, name="warm_in")
-        warm_out = keep.tile([P, 1], F32, name="warm_out")
-        nc.vector.memset(warm_in[:], 0.0)
-        nc.scalar.activation(warm_out[:], warm_in[:], GELU)
         identity = keep.tile([P, P], F32, name="identity", align_bytes=64)
         make_identity(nc, identity[:])
 

@@ -81,16 +81,20 @@ def tile_picked_zmae_lingelu_po_kernel(
         identity = keep.tile([P, P], F32, name="identity", align_bytes=64)
         make_identity(nc, identity[:])
 
-        lead_bf = [keep.tile([P, PASSES * K_PASS], BF16, name=f"lead_bf{h}", align_bytes=64) for h in range(2)]
-        late_bf = keep.tile([P, 2 * PASSES * K_PASS], BF16, name="late_bf", align_bytes=64)
+        lead_bf = {
+            (h, g): keep.tile([P, K_PASS], BF16, name=f"lead_bf{h}_{g}", align_bytes=64)
+            for h in range(2)
+            for g in range(PASSES)
+        }
+        late_bf = [keep.tile([P, 2 * K_PASS], BF16, name=f"late_bf{g}", align_bytes=64) for g in range(PASSES)]
 
         def cast_lead(copy, h, g):
-            dst = lead_bf[h][:].rearrange("p (g i u j) -> p g i j u", g=PASSES, u=2, j=PACK)
-            copy(dst[:, g], w_raw[h, g][:, :, :, 0:2])
+            dst = lead_bf[h, g][:].rearrange("p (i u j) -> p i j u", u=2, j=PACK)
+            copy(dst, w_raw[h, g][:, :, :, 0:2])
 
         def cast_late(h, g):
-            dst = late_bf[:].rearrange("p (g t h i j) -> p g h i j t", g=PASSES, t=2, h=2, j=PACK)
-            nc.scalar.copy(dst[:, g, h], w_raw[h, g][:, :, :, 2:4])
+            dst = late_bf[g][:].rearrange("p (t h i j) -> p h i j t", t=2, h=2, j=PACK)
+            nc.scalar.copy(dst[:, h], w_raw[h, g][:, :, :, 2:4])
 
         def quantize_w(name, rounded):
             width = rounded.shape[1] // PACK
@@ -98,6 +102,9 @@ def tile_picked_zmae_lingelu_po_kernel(
             scales = keep.tile([P, width], U8, name=f"{name}_scales", align_bytes=64)
             nc.vector.quantize_mx(out=codes[:].bitcast(FP8X4), scales=scales[:], in_=rounded[:])
             return codes, scales
+
+        def quantize_lead(h):
+            return [quantize_w(f"lead{h}_{g}", lead_bf[h, g]) for g in range(PASSES)]
 
         x_codes = [keep.tile([P, S], U32, name=f"x_codes{g}", align_bytes=64) for g in range(PASSES)]
         x_bytes = keep.tile([P, S], U8, name="x_bytes", align_bytes=64)
@@ -108,19 +115,19 @@ def tile_picked_zmae_lingelu_po_kernel(
             return psum.tile(shape, F32, name=name, tag=f"bank{n}")
 
         def product(u, a, b, weights, col, n, y=None):
-            codes, scales = weights
-            stride = codes.shape[1] // PASSES
             acc = bank(n, f"acc{u}_{a}", [P, b - a])
-            for g in range(PASSES):
-                cols = slice(g * stride + col, g * stride + col + P)
+            order = (0, 1) if u == 0 else (1, 0)
+            for g in order:
+                codes, scales = weights[g]
+                cols = slice(col, col + P)
                 nc.tensor.matmul_mx(
                     out=acc[:],
                     lhsT=codes[:, cols].bitcast(FP8X4),
                     lhsT_scale=scales[:, cols],
                     rhs=x_codes[g][:, a:b].bitcast(FP8X4),
                     rhs_scale=x_bytes[4 * g : P, a:b],
-                    start=(g == 0),
-                    stop=(g == PASSES - 1),
+                    start=(g == order[0]),
+                    stop=(g == order[-1]),
                 )
             nc.scalar.activation(ys[u][:, a:b] if y is None else y, acc[:], GELU)
 
@@ -133,7 +140,7 @@ def tile_picked_zmae_lingelu_po_kernel(
         nc.vector.tensor_copy(x_bytes[:], scale_table[:].indirect(offsets[:]))
         cast_lead(nc.scalar.copy, 0, 0)
         cast_lead(nc.vector.tensor_copy, 0, 1)
-        lead0 = quantize_w("lead0", lead_bf[0])
+        lead0 = quantize_lead(0)
         cast_late(0, 0)
         cast_late(0, 1)
         for a, b in ((0, LEAD), (LEAD, S - LEAD), (S - LEAD, S)):
@@ -145,10 +152,11 @@ def tile_picked_zmae_lingelu_po_kernel(
 
         for g in range(PASSES):
             cast_lead(nc.scalar.copy, 1, g)
-        lead1 = quantize_w("lead1", lead_bf[1])
+        lead1 = quantize_lead(1)
+        late = []
         for g in range(PASSES):
             cast_late(1, g)
-        late = quantize_w("late", late_bf)
+            late.append(quantize_w(f"late{g}", late_bf[g]))
         y_rest = keep.tile([P, LEAD], F32, name="y_rest", tag="last_rows", align_bytes=64)
         product(0, S - LEAD, S, lead0, 0, 2, y_rest[:])
         scatter(0, S - LEAD, S, y_rest[:])

@@ -48,7 +48,11 @@ def tile_picked_zmae_lingelu_po_kernel(
             tag = "last_rows" if (h, g) == (1, PASSES - 1) else f"w_raw{h}_{g}"
             raw = keep.tile([P, PACK, M // 2], F32, name=f"w_raw{h}_{g}", tag=tag, align_bytes=64)
             rows = w1[g * K_PASS : (g + 1) * K_PASS, h * M // 2 : (h + 1) * M // 2]
-            nc.sync.dma_start(raw[:], rows.rearrange("(p j) c -> p j c", j=PACK))
+            parts = 2 if (h, g) == (1, PASSES - 1) else 1
+            width = M // 2 // parts
+            for part in range(parts):
+                at = slice(part * width, (part + 1) * width)
+                nc.sync.dma_start(raw[:, :, at], rows.rearrange("(p j) c -> p j c", j=PACK)[:, :, at])
             return raw[:].rearrange("p j (i t) -> p i j t", t=PACK)
 
         def load_x(g, queue):
@@ -86,25 +90,25 @@ def tile_picked_zmae_lingelu_po_kernel(
             for h in range(2)
             for g in range(PASSES)
         }
-        late_bf = [keep.tile([P, 2 * K_PASS], BF16, name=f"late_bf{g}", align_bytes=64) for g in range(PASSES)]
+        late_bf = keep.tile([P, 2 * PASSES * K_PASS], BF16, name="late_bf", align_bytes=64)
 
-        def cast_lead(copy, h, g):
+        def cast_lead(copy, h, g, i0=0, i1=HALF):
             dst = lead_bf[h, g][:].rearrange("p (i u j) -> p i j u", u=2, j=PACK)
-            copy(dst, w_raw[h, g][:, :, :, 0:2])
+            copy(dst[:, i0:i1], w_raw[h, g][:, i0:i1, :, 0:2])
 
-        def cast_late(h, g):
-            dst = late_bf[g][:].rearrange("p (t h i j) -> p h i j t", t=2, h=2, j=PACK)
-            nc.scalar.copy(dst[:, h], w_raw[h, g][:, :, :, 2:4])
+        def cast_late(h, g, i0=0, i1=HALF):
+            dst = late_bf[:].rearrange("p (t g h i j) -> p g h i j t", t=2, g=PASSES, h=2, j=PACK)
+            nc.scalar.copy(dst[:, g, h, i0:i1], w_raw[h, g][:, i0:i1, :, 2:4])
 
-        def quantize_w(name, rounded):
+        def quantize_w(name, rounded, tag=None):
             width = rounded.shape[1] // PACK
-            codes = keep.tile([P, width], U32, name=f"{name}_codes", align_bytes=64)
+            codes = keep.tile([P, width], U32, name=f"{name}_codes", tag=tag or f"{name}_codes", align_bytes=64)
             scales = keep.tile([P, width], U8, name=f"{name}_scales", align_bytes=64)
-            nc.vector.quantize_mx(out=codes[:].bitcast(FP8X4), scales=scales[:], in_=rounded[:])
-            return codes, scales
+            nc.vector.quantize_mx(out=codes[:].bitcast(FP8X4), scales=scales[:], in_=rounded)
+            return codes[:], scales[:]
 
         def quantize_lead(h):
-            return [quantize_w(f"lead{h}_{g}", lead_bf[h, g]) for g in range(PASSES)]
+            return [quantize_w(f"lead{h}_{g}", lead_bf[h, g][:]) for g in range(PASSES)]
 
         x_codes = [keep.tile([P, S], U32, name=f"x_codes{g}", align_bytes=64) for g in range(PASSES)]
         x_bytes = keep.tile([P, S], U8, name="x_bytes", align_bytes=64)
@@ -150,21 +154,25 @@ def tile_picked_zmae_lingelu_po_kernel(
         scatter(0, 0, LEAD)
         scatter(0, LEAD, S - LEAD)
 
-        for g in range(PASSES):
-            cast_lead(nc.scalar.copy, 1, g)
+        cast_lead(nc.scalar.copy, 1, 0)
+        for i0 in (0, HALF // 2):
+            cast_lead(nc.scalar.copy, 1, 1, i0, i0 + HALF // 2)
         lead1 = quantize_lead(1)
-        late = []
-        for g in range(PASSES):
-            cast_late(1, g)
-            late.append(quantize_w(f"late{g}", late_bf[g]))
+        cast_late(1, 0)
+        third = [quantize_w("third0", late_bf[:, :K_PASS])]
+        for i0 in (0, HALF // 2):
+            cast_late(1, 1, i0, i0 + HALF // 2)
+        third.append(quantize_w("third1", late_bf[:, K_PASS : 2 * K_PASS]))
         y_rest = keep.tile([P, LEAD], F32, name="y_rest", tag="last_rows", align_bytes=64)
         product(0, S - LEAD, S, lead0, 0, 2, y_rest[:])
         scatter(0, S - LEAD, S, y_rest[:])
         for n, (a, b) in enumerate(slices):
             product(1, a, b, lead1, 0, 3 + n)
-        product(2, 0, S, late, 0, 6)
-        product(3, 0, S, late, P, 7)
+        product(2, 0, S, third, 0, 6)
         scatter(1, 0, LEAD)
+        codes, scales = quantize_w("fourth", late_bf[:, 2 * K_PASS :], "last_rows")
+        fourth = [(codes[:, g * P : (g + 1) * P], scales[:, g * P : (g + 1) * P]) for g in range(PASSES)]
+        product(3, 0, S, fourth, 0, 7)
         scatter(1, LEAD, S)
         scatter(2, 0, S)
         scatter(3, 0, S)

@@ -36,7 +36,6 @@ def tile_picked_zmae_lingelu_po_kernel(
         psum = ctx.enter_context(tc.psum_pool(name="psum", bufs=1))
 
         offsets = keep.tile([P, S // LIST_ROWS], U16, name="offsets")
-        nc.sync.dma_start(offsets[:], offs)
 
         def picks(a, b):
             return offsets[:, a // LIST_ROWS : b // LIST_ROWS]
@@ -45,14 +44,9 @@ def tile_picked_zmae_lingelu_po_kernel(
         nc.gpsimd.memset(scale_table[:].bitcast(I32), 0)
 
         def load_w(h, g):
-            tag = "last_rows" if (h, g) == (1, PASSES - 1) else f"w_raw{h}_{g}"
-            raw = keep.tile([P, PACK, M // 2], F32, name=f"w_raw{h}_{g}", tag=tag, align_bytes=64)
+            raw = keep.tile([P, PACK, M // 2], F32, name=f"w_raw{h}_{g}", tag=f"w_raw{h}_{g}", align_bytes=64)
             rows = w1[g * K_PASS : (g + 1) * K_PASS, h * M // 2 : (h + 1) * M // 2]
-            parts = 2 if (h, g) == (1, PASSES - 1) else 1
-            width = M // 2 // parts
-            for part in range(parts):
-                at = slice(part * width, (part + 1) * width)
-                nc.sync.dma_start(raw[:, :, at], rows.rearrange("(p j) c -> p j c", j=PACK)[:, :, at])
+            nc.sync.dma_start(raw[:], rows.rearrange("(p j) c -> p j c", j=PACK))
             return raw[:].rearrange("p j (i t) -> p i j t", t=PACK)
 
         def load_x(g, queue):
@@ -70,7 +64,8 @@ def tile_picked_zmae_lingelu_po_kernel(
             nc.sync.dma_start(window[:], rows_of(mask, u))
             return window
 
-        x0 = load_x(0, nc.scalar)
+        x0 = load_x(0, nc.sync)
+        nc.sync.dma_start(offsets[:], offs)
         w_raw = {(0, 0): load_w(0, 0)}
         for q in range(4):
             live = slice(32 * q, 32 * q + 4 * PASSES)
@@ -78,15 +73,15 @@ def tile_picked_zmae_lingelu_po_kernel(
         w_raw[0, 1] = load_w(0, 1)
         x1 = load_x(1, nc.sync)
         windows = [load_window(0)]
-        for g in range(PASSES):
-            w_raw[1, g] = load_w(1, g)
+        w_raw[1, 0] = load_w(1, 0)
+        w_raw[1, 1] = load_w(1, 1)
         windows.extend(load_window(u) for u in range(1, PACK))
 
         identity = keep.tile([P, P], F32, name="identity", align_bytes=64)
         make_identity(nc, identity[:])
 
         lead_bf = {
-            (h, g): keep.tile([P, K_PASS], BF16, name=f"lead_bf{h}_{g}", align_bytes=64)
+            (h, g): keep.tile([P, K_PASS], BF16, name=f"lead_bf{h}_{g}", tag=f"lead_bf{h}_{g}", align_bytes=64)
             for h in range(2)
             for g in range(PASSES)
         }
@@ -120,7 +115,7 @@ def tile_picked_zmae_lingelu_po_kernel(
 
         def product(u, a, b, weights, col, n, y=None):
             acc = bank(n, f"acc{u}_{a}", [P, b - a])
-            order = (0, 1) if u == 0 else (1, 0)
+            order = (0, 1) if u == 0 or (u, a) == (1, 0) else (1, 0)
             for g in order:
                 codes, scales = weights[g]
                 cols = slice(col, col + P)
@@ -155,23 +150,22 @@ def tile_picked_zmae_lingelu_po_kernel(
         scatter(0, LEAD, S - LEAD)
 
         cast_lead(nc.scalar.copy, 1, 0)
-        for i0 in (0, HALF // 2):
-            cast_lead(nc.scalar.copy, 1, 1, i0, i0 + HALF // 2)
-        lead1 = quantize_lead(1)
+        lead1 = [quantize_w("lead1_0", lead_bf[1, 0][:])]
         cast_late(1, 0)
+        cast_lead(nc.scalar.copy, 1, 1)
         third = [quantize_w("third0", late_bf[:, :K_PASS])]
-        for i0 in (0, HALF // 2):
-            cast_late(1, 1, i0, i0 + HALF // 2)
-        third.append(quantize_w("third1", late_bf[:, K_PASS : 2 * K_PASS]))
-        y_rest = keep.tile([P, LEAD], F32, name="y_rest", tag="last_rows", align_bytes=64)
+        lead1.append(quantize_w("lead1_1", lead_bf[1, 1][:]))
+        y_rest = keep.tile([P, LEAD], F32, name="y_rest", tag="w_raw1_0", align_bytes=64)
         product(0, S - LEAD, S, lead0, 0, 2, y_rest[:])
         scatter(0, S - LEAD, S, y_rest[:])
+        cast_late(1, 1)
         for n, (a, b) in enumerate(slices):
             product(1, a, b, lead1, 0, 3 + n)
-        product(2, 0, S, third, 0, 6)
-        scatter(1, 0, LEAD)
-        codes, scales = quantize_w("fourth", late_bf[:, 2 * K_PASS :], "last_rows")
+        codes, scales = quantize_w("fourth", late_bf[:, 2 * K_PASS :])
         fourth = [(codes[:, g * P : (g + 1) * P], scales[:, g * P : (g + 1) * P]) for g in range(PASSES)]
+        scatter(1, 0, LEAD)
+        third.append(quantize_w("third1", late_bf[:, K_PASS : 2 * K_PASS]))
+        product(2, 0, S, third, 0, 6)
         product(3, 0, S, fourth, 0, 7)
         scatter(1, LEAD, S)
         scatter(2, 0, S)
@@ -182,63 +176,51 @@ def tile_picked_zmae_lingelu_po_kernel(
             stage.tile([P, blocks, 2 * P], BF16, name=f"turned{k}", align_bytes=64, offset=4096 * k + 1024)
             for k in range(2)
         ]
-        for u, first_bank in ((0, 3), (1, 6)):
-            for k in (1, 0):
-                across = bank(first_bank + k, f"across{u}_{k}", [P, blocks, P])
-                for b in range(blocks):
-                    c0 = k * BANK + b * P
-                    nc.tensor.transpose(across[:, b, :], windows[u][:, c0 : c0 + P], identity[:])
-                nc.scalar.copy(turned[k][:, :, u * P : (u + 1) * P], across[:])
+        for u, k, b0, b1, n in ((0, 1, 0, 4, 4), (0, 0, 0, 4, 3), (1, 1, 0, 2, 7), (1, 1, 2, 4, 6), (1, 0, 0, 4, 5)):
+            across = bank(n, f"across{u}_{k}_{b0}", [P, b1 - b0, P])
+            for b in range(b0, b1):
+                c0 = k * BANK + b * P
+                nc.tensor.transpose(across[:, b - b0, :], windows[u][:, c0 : c0 + P], identity[:])
+            nc.scalar.copy(turned[k][:, b0:b1, u * P : (u + 1) * P], across[:])
 
-        pairs = {}
-        for k in (1, 0):
+        def turn_back(k):
             back = bank(k, f"back{k}", [P, blocks, P])
             for b in range(blocks):
                 nc.tensor.transpose(back[:, b, :], turned[k][:, b, :].bitcast(F32), identity[:])
-            pairs[k] = stage.tile([P, 2, 2 * BANK], BF16, name=f"pairs{k}", align_bytes=64, offset=4096 * k)
-            nc.scalar.copy(pairs[k][:, 0, :].bitcast(F32), back[:].rearrange("p b c -> p (b c)"))
-        for k in (1, 0):
-            plane = windows[2][:, k * BANK : (k + 1) * BANK].rearrange("p (h c) -> p h c", h=2)
-            uppers = pairs[k][:, 1, :].rearrange("p (h c e) -> p h c e", h=2, e=2)
-            nc.scalar.copy(uppers[:, :, 1:, 0], plane[:, :, 1:])
-            nc.scalar.copy(uppers[:, :, 0, :], plane[:, :, 0:1].to_broadcast([P, 2, 2]))
+            return back[:].rearrange("p b c -> p (b c)")
 
-        def within(c):
-            return slice((c % 2) * CHUNK, (c % 2 + 1) * CHUNK)
+        direct = keep.tile([P, BANK * PACK], BF16, name="direct", align_bytes=64)
+        direct_words = direct[:].bitcast(F32).rearrange("p (c u) -> p c u", u=2)
+        nc.scalar.copy(direct_words, turn_back(1).unsqueeze(2).to_broadcast([P, BANK, 2]))
+        back = turn_back(0)
+        pairs = stage.tile([P, 2, 2 * BANK], BF16, name="pairs", align_bytes=64, offset=0)
+        nc.scalar.copy(pairs[:, 0, :].bitcast(F32), back)
+        plane = windows[2][:, :BANK].rearrange("p (h c) -> p h c", h=2)
+        uppers = pairs[:, 1, :].rearrange("p (h c e) -> p h c e", h=2, e=2)
+        nc.scalar.copy(uppers[:, :, 1:, 0], plane[:, :, 1:])
+        nc.scalar.copy(uppers[:, :, 0, :], plane[:, :, 0:1].to_broadcast([P, 2, 2]))
+        slots = direct[:].rearrange("p (c t) -> p c t", t=PACK)
+        nc.scalar.copy(slots[:, :, 2], windows[2][:, BANK:])
 
-        def upper(c):
-            return pairs[c // 2][:, 1, :].rearrange("p (c e) -> p c e", e=2)[:, within(c), :]
-
-        def cols(u, c):
-            return windows[u][:, c * CHUNK : (c + 1) * CHUNK]
+        def chunk(c):
+            return slice(c * CHUNK, (c + 1) * CHUNK)
 
         out_codes = keep.tile([P, T], U32, name="out_codes", align_bytes=64)
         out_scales = keep.tile([P, T], U8, name="out_scales", align_bytes=64)
         words = out_1[0].rearrange("p n t -> p (n t)").bitcast(I32)
-        woven = [keep.tile([P, CHUNK * PACK], BF16, name=f"woven{c}", align_bytes=64) for c in range(T // CHUNK)]
+        woven = [keep.tile([P, CHUNK * PACK], BF16, name=f"woven{c}", align_bytes=64) for c in range(2)]
+        both = pairs[:].rearrange("p u (c e) -> p c u e", e=2)
 
-        def weave(copy, c):
-            copy(
-                woven[c][:].rearrange("p (c u e) -> p c u e", u=2, e=2),
-                pairs[c // 2][:].rearrange("p u (c e) -> p c u e", e=2)[:, within(c)],
-            )
-
-        def weave_words(c):
-            nc.scalar.copy(
-                woven[c][:].bitcast(U32).rearrange("p (c u) -> p c u", u=2),
-                pairs[c // 2][:].bitcast(U32)[:, :, within(c)].rearrange("p u c -> p c u"),
-            )
-
-        nc.scalar.copy(upper(2)[:, :, 1], cols(3, 2))
-        for c in (3, 0, 1):
-            nc.vector.tensor_copy(upper(c)[:, :, 1], cols(3, c))
-        for c in (2, 3):
-            weave_words(c)
-        for c in (0, 1):
-            weave(nc.vector.tensor_copy, c)
+        for c in range(2):
+            nc.scalar.copy(slots[:, chunk(c), 3], windows[3][:, chunk(2 + c)])
+        for c in range(2):
+            nc.vector.tensor_copy(both[:, chunk(c), 1, 1], windows[3][:, chunk(c)])
+        for c in range(2):
+            nc.vector.tensor_copy(woven[c][:].rearrange("p (c u e) -> p c u e", u=2, e=2), both[:, chunk(c)])
+        rounded = [woven[0][:], woven[1][:], direct[:, : CHUNK * PACK], direct[:, CHUNK * PACK :]]
         for c in range(T // CHUNK):
-            at = slice(c * CHUNK, (c + 1) * CHUNK)
-            nc.vector.quantize_mx(out=out_codes[:, at].bitcast(FP8X4), scales=out_scales[:, at], in_=woven[c][:])
+            at = chunk(c)
+            nc.vector.quantize_mx(out=out_codes[:, at].bitcast(FP8X4), scales=out_scales[:, at], in_=rounded[c])
             if c > 0:
                 stored = slice(0, 2 * CHUNK) if c == 1 else at
                 nc.sync.dma_start(words[:, stored], out_codes[:, stored].bitcast(I32))

@@ -1,7 +1,6 @@
 from contextlib import ExitStack
 
 import concourse.mybir as mybir
-from concourse.masks import make_identity
 
 K, T, S, M = 1024, 1024, 512, 512
 FLOPS = 2 * K * S * M
@@ -14,16 +13,14 @@ U16 = mybir.dt.uint16
 U8 = mybir.dt.uint8
 FP8X4 = mybir.dt.float8_e4m3fn_x4
 GELU = mybir.ActivationFunctionType.Gelu_apprx_tanh
+COPY = mybir.ActivationFunctionType.Copy
 
 P = 128
 PACK = 4
 K_PASS = P * PACK
 PASSES = K // K_PASS
 LIST_ROWS = 16
-HALF = P // 2
-LEAD = 128
-CHUNK = 256
-BANK = 512
+SPLIT = 384
 
 
 def tile_picked_zmae_lingelu_po_kernel(
@@ -32,7 +29,7 @@ def tile_picked_zmae_lingelu_po_kernel(
     nc = tc.nc
     with ExitStack() as ctx:
         keep = ctx.enter_context(tc.tile_pool(name="keep", bufs=1))
-        stage = ctx.enter_context(tc.tile_pool(name="stage", bufs=1))
+        reused = ctx.enter_context(tc.tile_pool(name="reused", bufs=1))
         psum = ctx.enter_context(tc.psum_pool(name="psum", bufs=1))
 
         offsets = keep.tile([P, S // LIST_ROWS], U16, name="offsets")
@@ -43,187 +40,149 @@ def tile_picked_zmae_lingelu_po_kernel(
         scale_table = keep.tile([P, T], U8, name="scale_table", align_bytes=64)
         nc.gpsimd.memset(scale_table[:].bitcast(I32), 0)
 
-        def load_w(h, g):
-            raw = keep.tile([P, PACK, M // 2], F32, name=f"w_raw{h}_{g}", tag=f"w_raw{h}_{g}", align_bytes=64)
-            rows = w1[g * K_PASS : (g + 1) * K_PASS, h * M // 2 : (h + 1) * M // 2]
+        def load_w(g):
+            raw = reused.tile([P, PACK, M], F32, name=f"w_raw{g}", align_bytes=64, offset=8192 * g)
+            rows = w1[g * K_PASS : (g + 1) * K_PASS, :]
             nc.sync.dma_start(raw[:], rows.rearrange("(p j) c -> p j c", j=PACK))
-            return raw[:].rearrange("p j (i t) -> p i j t", t=PACK)
+            return raw[:].rearrange("p j (m t) -> p m j t", t=PACK)
 
-        def load_x(g, queue):
+        def load_x(g):
             table = keep.tile([P, T], U32, name=f"word_table{g}", align_bytes=64)
             words_in = x_words[g].rearrange("p n t -> p (n t)").bitcast(I32)
-            queue.dma_start(table[:].bitcast(I32), words_in)
+            nc.sync.dma_start(table[:].bitcast(I32), words_in)
             return table
 
-        def rows_of(dram, u):
-            dealt = dram.rearrange("(p t) c -> p t c", t=PACK)
-            return dealt[u * HALF : (u + 1) * HALF, 0:2, :] if u < 2 else dealt[:, u, :]
+        def rows_of(dram, t):
+            return dram.rearrange("(p t) c -> p t c", t=PACK)[:, t, :]
 
-        def load_window(u):
-            window = keep.tile([P, T], F32, name=f"window{u}", align_bytes=64)
-            nc.sync.dma_start(window[:], rows_of(mask, u))
+        def load_window(t):
+            if t % 2 == 0:
+                window = keep.tile([P, T], F32, name=f"window{t}", align_bytes=64)
+                nc.sync.dma_start(window[:], rows_of(mask, t))
+            else:
+                window = reused.tile([P, T], F32, name=f"window{t}", align_bytes=64, offset=8192 + 4096 * (t // 2))
+                nc.scalar.dma_start(window[:], rows_of(mask, t))
             return window
 
-        x0 = load_x(0, nc.sync)
+        x0 = load_x(0)
         nc.sync.dma_start(offsets[:], offs)
-        w_raw = {(0, 0): load_w(0, 0)}
         for q in range(4):
             live = slice(32 * q, 32 * q + 4 * PASSES)
             nc.sync.dma_start(scale_table[live, :].bitcast(I32), x_scales[:, 4 * q : 4 * q + 4, :].bitcast(I32))
-        w_raw[0, 1] = load_w(0, 1)
-        x1 = load_x(1, nc.sync)
-        windows = [load_window(0)]
-        w_raw[1, 0] = load_w(1, 0)
-        w_raw[1, 1] = load_w(1, 1)
-        windows.extend(load_window(u) for u in range(1, PACK))
+        w_raw = [load_w(g) for g in range(PASSES)]
+        x1 = load_x(1)
+        windows = {t: load_window(t) for t in (0, 2)}
 
-        identity = keep.tile([P, P], F32, name="identity", align_bytes=64)
-        make_identity(nc, identity[:])
+        def round_w(copy, g, h):
+            rounded = keep.tile([P, 2 * K_PASS], BF16, name=f"w_bf{g}_{h}", align_bytes=64)
+            copy(rounded[:].rearrange("p (t m j) -> p m j t", t=2, j=PACK), w_raw[g][:, :, :, 2 * h : 2 * h + 2])
+            return rounded
 
-        lead_bf = {
-            (h, g): keep.tile([P, K_PASS], BF16, name=f"lead_bf{h}_{g}", tag=f"lead_bf{h}_{g}", align_bytes=64)
-            for h in range(2)
-            for g in range(PASSES)
-        }
-        late_bf = keep.tile([P, 2 * PASSES * K_PASS], BF16, name="late_bf", align_bytes=64)
-
-        def cast_lead(copy, h, g, i0=0, i1=HALF):
-            dst = lead_bf[h, g][:].rearrange("p (i u j) -> p i j u", u=2, j=PACK)
-            copy(dst[:, i0:i1], w_raw[h, g][:, i0:i1, :, 0:2])
-
-        def cast_late(h, g, i0=0, i1=HALF):
-            dst = late_bf[:].rearrange("p (t g h i j) -> p g h i j t", t=2, g=PASSES, h=2, j=PACK)
-            nc.scalar.copy(dst[:, g, h, i0:i1], w_raw[h, g][:, i0:i1, :, 2:4])
-
-        def quantize_w(name, rounded, tag=None):
-            width = rounded.shape[1] // PACK
-            codes = keep.tile([P, width], U32, name=f"{name}_codes", tag=tag or f"{name}_codes", align_bytes=64)
-            scales = keep.tile([P, width], U8, name=f"{name}_scales", align_bytes=64)
-            nc.vector.quantize_mx(out=codes[:].bitcast(FP8X4), scales=scales[:], in_=rounded)
-            return codes[:], scales[:]
-
-        def quantize_lead(h):
-            return [quantize_w(f"lead{h}_{g}", lead_bf[h, g][:]) for g in range(PASSES)]
+        def quantize_w(g, h, rounded):
+            codes = keep.tile([P, 2 * P], U32, name=f"w_codes{g}_{h}", align_bytes=64)
+            scales = keep.tile([P, 2 * P], U8, name=f"w_scales{g}_{h}", align_bytes=64)
+            nc.vector.quantize_mx(out=codes[:].bitcast(FP8X4), scales=scales[:], in_=rounded[:])
+            return codes, scales
 
         x_codes = [keep.tile([P, S], U32, name=f"x_codes{g}", align_bytes=64) for g in range(PASSES)]
         x_bytes = keep.tile([P, S], U8, name="x_bytes", align_bytes=64)
-        slices = ((0, LEAD), (LEAD, 2 * LEAD), (2 * LEAD, S))
-        ys = [keep.tile([P, S], F32, name=f"y{u}", align_bytes=64) for u in range(PACK)]
+        half = S // 2
+        slices = ((0, half), (half, S))
+        weights = {}
 
-        def bank(n, name, shape):
-            return psum.tile(shape, F32, name=name, tag=f"bank{n}")
+        def products(name, parts):
+            width = sum(b - a for t, a, b in parts)
+            acc = psum.tile([P, width], F32, name=f"acc_{name}")
+            for g in range(PASSES):
+                at = 0
+                for n, (t, a, b) in enumerate(parts):
+                    codes, scales = weights[g, t // 2]
+                    cols = slice(t % 2 * P, (t % 2 + 1) * P)
+                    nc.tensor.matmul_mx(
+                        out=acc[:, at : at + b - a],
+                        lhsT=codes[:, cols].bitcast(FP8X4),
+                        lhsT_scale=scales[:, cols],
+                        rhs=x_codes[g][:, a:b].bitcast(FP8X4),
+                        rhs_scale=x_bytes[4 * g : P, a:b],
+                        start=(g == 0 and n == 0),
+                        stop=(g == PASSES - 1 and n == len(parts) - 1),
+                    )
+                    at = at + b - a
+            y = keep.tile([P, width], F32, name=f"y_{name}", tag=f"y_{name}", align_bytes=64)
+            nc.scalar.activation(y[:], acc[:], GELU)
+            return y
 
-        def product(u, a, b, weights, col, n, y=None):
-            acc = bank(n, f"acc{u}_{a}", [P, b - a])
-            order = (0, 1) if u == 0 or (u, a) == (1, 0) else (1, 0)
-            for g in order:
-                codes, scales = weights[g]
-                cols = slice(col, col + P)
-                nc.tensor.matmul_mx(
-                    out=acc[:],
-                    lhsT=codes[:, cols].bitcast(FP8X4),
-                    lhsT_scale=scales[:, cols],
-                    rhs=x_codes[g][:, a:b].bitcast(FP8X4),
-                    rhs_scale=x_bytes[4 * g : P, a:b],
-                    start=(g == order[0]),
-                    stop=(g == order[-1]),
-                )
-            nc.scalar.activation(ys[u][:, a:b] if y is None else y, acc[:], GELU)
-
-        def scatter(u, a, b, y=None):
-            nc.vector.tensor_copy(windows[u][:].indirect(picks(a, b)), ys[u][:, a:b] if y is None else y)
+        def scatter(t, a, b, y):
+            window = windows[t][:].indirect(picks(a, b))
+            if t < 2:
+                nc.vector.tensor_copy(window, y)
+            else:
+                nc.scalar.activation(window, y, COPY)
             if b == S:
-                nc.sync.dma_start(rows_of(out_0, u), windows[u][:])
+                nc.sync.dma_start(rows_of(out_0, t), windows[t][:])
 
         nc.vector.tensor_copy(x_codes[0][:], x0[:].indirect(offsets[:]))
         nc.vector.tensor_copy(x_bytes[:], scale_table[:].indirect(offsets[:]))
-        cast_lead(nc.scalar.copy, 0, 0)
-        cast_lead(nc.vector.tensor_copy, 0, 1)
-        lead0 = quantize_lead(0)
-        cast_late(0, 0)
-        cast_late(0, 1)
-        for a, b in ((0, LEAD), (LEAD, S - LEAD), (S - LEAD, S)):
+        first = [round_w(nc.vector.tensor_copy, 0, 0), round_w(nc.scalar.copy, 0, 1)]
+        for h in range(2):
+            weights[0, h] = quantize_w(0, h, first[h])
+        second = [round_w(nc.vector.tensor_copy, 1, 0), round_w(nc.scalar.copy, 1, 1)]
+        windows.update({t: load_window(t) for t in (1, 3)})
+        weights[1, 0] = quantize_w(1, 0, second[0])
+        for a, b in slices:
             nc.vector.tensor_copy(x_codes[1][:, a:b], x1[:].indirect(picks(a, b)))
-        product(0, 0, LEAD, lead0, 0, 0)
-        product(0, LEAD, S - LEAD, lead0, 0, 1)
-        scatter(0, 0, LEAD)
-        scatter(0, LEAD, S - LEAD)
+            if b == half:
+                weights[1, 1] = quantize_w(1, 1, second[1])
+        lead = [products(f"lead{t}", [(t, 0, half)]) for t in range(2)]
+        front = products("front", [(2, 0, half), (3, 0, half)])
+        rest = products("rest", [(0, half, S), (1, half, S)])
+        back = products("back", [(2, half, S), (3, half, S)])
+        for t in range(2):
+            scatter(t, 0, half, lead[t][:])
+        for t in range(2):
+            scatter(t, half, S, rest[:, t * half : (t + 1) * half])
+        for t in range(2):
+            scatter(2 + t, 0, half, front[:, t * half : (t + 1) * half])
+        for t in range(2):
+            scatter(2 + t, half, S, back[:, t * half : (t + 1) * half])
 
-        cast_lead(nc.scalar.copy, 1, 0)
-        lead1 = [quantize_w("lead1_0", lead_bf[1, 0][:])]
-        cast_late(1, 0)
-        cast_lead(nc.scalar.copy, 1, 1)
-        third = [quantize_w("third0", late_bf[:, :K_PASS])]
-        lead1.append(quantize_w("lead1_1", lead_bf[1, 1][:]))
-        y_rest = keep.tile([P, LEAD], F32, name="y_rest", tag="w_raw1_0", align_bytes=64)
-        product(0, S - LEAD, S, lead0, 0, 2, y_rest[:])
-        scatter(0, S - LEAD, S, y_rest[:])
-        cast_late(1, 1)
-        for n, (a, b) in enumerate(slices):
-            product(1, a, b, lead1, 0, 3 + n)
-        codes, scales = quantize_w("fourth", late_bf[:, 2 * K_PASS :])
-        fourth = [(codes[:, g * P : (g + 1) * P], scales[:, g * P : (g + 1) * P]) for g in range(PASSES)]
-        scatter(1, 0, LEAD)
-        third.append(quantize_w("third1", late_bf[:, K_PASS : 2 * K_PASS]))
-        product(2, 0, S, third, 0, 6)
-        product(3, 0, S, fourth, 0, 7)
-        scatter(1, LEAD, S)
-        scatter(2, 0, S)
-        scatter(3, 0, S)
-
-        blocks = BANK // P
-        turned = [
-            stage.tile([P, blocks, 2 * P], BF16, name=f"turned{k}", align_bytes=64, offset=4096 * k + 1024)
-            for k in range(2)
+        spans = ((0, SPLIT), (SPLIT, T))
+        pairs = [
+            keep.tile([P, 2, b - a, 2], BF16, name=f"pairs{n}", align_bytes=64)
+            for n, (a, b) in enumerate(spans)
         ]
-        for u, k, b0, b1, n in ((0, 1, 0, 4, 4), (0, 0, 0, 4, 3), (1, 1, 0, 2, 7), (1, 1, 2, 4, 6), (1, 0, 0, 4, 5)):
-            across = bank(n, f"across{u}_{k}_{b0}", [P, b1 - b0, P])
-            for b in range(b0, b1):
-                c0 = k * BANK + b * P
-                nc.tensor.transpose(across[:, b - b0, :], windows[u][:, c0 : c0 + P], identity[:])
-            nc.scalar.copy(turned[k][:, b0:b1, u * P : (u + 1) * P], across[:])
 
-        def turn_back(k):
-            back = bank(k, f"back{k}", [P, blocks, P])
-            for b in range(blocks):
-                nc.tensor.transpose(back[:, b, :], turned[k][:, b, :].bitcast(F32), identity[:])
-            return back[:].rearrange("p b c -> p (b c)")
+        def round_plane(copy, t, n):
+            a, b = spans[n]
+            copy(pairs[n][:, t // 2, :, t % 2], windows[t][:, a:b])
 
-        direct = keep.tile([P, BANK * PACK], BF16, name="direct", align_bytes=64)
-        direct_words = direct[:].bitcast(F32).rearrange("p (c u) -> p c u", u=2)
-        nc.scalar.copy(direct_words, turn_back(1).unsqueeze(2).to_broadcast([P, BANK, 2]))
-        back = turn_back(0)
-        pairs = stage.tile([P, 2, 2 * BANK], BF16, name="pairs", align_bytes=64, offset=0)
-        nc.scalar.copy(pairs[:, 0, :].bitcast(F32), back)
-        plane = windows[2][:, :BANK].rearrange("p (h c) -> p h c", h=2)
-        uppers = pairs[:, 1, :].rearrange("p (h c e) -> p h c e", h=2, e=2)
-        nc.scalar.copy(uppers[:, :, 1:, 0], plane[:, :, 1:])
-        nc.scalar.copy(uppers[:, :, 0, :], plane[:, :, 0:1].to_broadcast([P, 2, 2]))
-        slots = direct[:].rearrange("p (c t) -> p c t", t=PACK)
-        nc.scalar.copy(slots[:, :, 2], windows[2][:, BANK:])
-
-        def chunk(c):
-            return slice(c * CHUNK, (c + 1) * CHUNK)
+        for n in range(2):
+            round_plane(nc.vector.tensor_copy, 0, n)
+        for n in range(2):
+            round_plane(nc.vector.tensor_copy, 1, n)
+        round_plane(nc.vector.tensor_copy, 2, 1)
+        round_plane(nc.scalar.copy, 2, 0)
+        round_plane(nc.scalar.copy, 3, 0)
+        round_plane(nc.vector.tensor_copy, 3, 1)
 
         out_codes = keep.tile([P, T], U32, name="out_codes", align_bytes=64)
         out_scales = keep.tile([P, T], U8, name="out_scales", align_bytes=64)
         words = out_1[0].rearrange("p n t -> p (n t)").bitcast(I32)
-        woven = [keep.tile([P, CHUNK * PACK], BF16, name=f"woven{c}", align_bytes=64) for c in range(2)]
-        both = pairs[:].rearrange("p u (c e) -> p c u e", e=2)
-
-        for c in range(2):
-            nc.scalar.copy(slots[:, chunk(c), 3], windows[3][:, chunk(2 + c)])
-        for c in range(2):
-            nc.vector.tensor_copy(both[:, chunk(c), 1, 1], windows[3][:, chunk(c)])
-        for c in range(2):
-            nc.vector.tensor_copy(woven[c][:].rearrange("p (c u e) -> p c u e", u=2, e=2), both[:, chunk(c)])
-        rounded = [woven[0][:], woven[1][:], direct[:, : CHUNK * PACK], direct[:, CHUNK * PACK :]]
-        for c in range(T // CHUNK):
-            at = chunk(c)
-            nc.vector.quantize_mx(out=out_codes[:, at].bitcast(FP8X4), scales=out_scales[:, at], in_=rounded[c])
-            if c > 0:
-                stored = slice(0, 2 * CHUNK) if c == 1 else at
-                nc.sync.dma_start(words[:, stored], out_codes[:, stored].bitcast(I32))
+        pieces = ((0, 0, 256), (0, 256, SPLIT), (1, SPLIT, 512), (1, 512, 768), (1, 768, T))
+        woven = {}
+        for n, a, b in pieces:
+            woven[a] = keep.tile([P, (b - a) * PACK], BF16, name=f"woven{a}", align_bytes=64)
+            dst = woven[a][:].rearrange("p (c u e) -> p c u e", u=2, e=2)
+            both = pairs[n][:].rearrange("p u c e -> p c u e")[:, a - spans[n][0] : b - spans[n][0]]
+            if n == 1:
+                nc.vector.tensor_copy(dst, both)
+            else:
+                nc.scalar.copy(dst.bitcast(F32), both.bitcast(F32))
+        for a, b in ((512, 768), (768, T), (SPLIT, 512), (0, 256), (256, SPLIT)):
+            nc.vector.quantize_mx(out=out_codes[:, a:b].bitcast(FP8X4), scales=out_scales[:, a:b], in_=woven[a][:])
+            if b == T:
+                nc.sync.dma_start(words[:, 512:], out_codes[:, 512:].bitcast(I32))
+        nc.sync.dma_start(words[:, :512], out_codes[:, :512].bitcast(I32))
         for q in range(4):
             queue = nc.sync if q % 2 == 0 else nc.scalar
             queue.dma_start(

@@ -40,6 +40,10 @@ def tile_picked_zmae_lingelu_po_kernel(
         scale_table = keep.tile([P, T], U8, name="scale_table", align_bytes=64)
         nc.gpsimd.memset(scale_table[:].bitcast(I32), 0)
 
+        warm = keep.tile([P, 2], F32, name="warm")
+        nc.vector.memset(warm[:], 0.0)
+        nc.scalar.activation(warm[:, 1:2], warm[:, 0:1], GELU)
+
         def load_w(g):
             raw = reused.tile([P, PACK, M], F32, name=f"w_raw{g}", align_bytes=64, offset=8192 * g)
             rows = w1[g * K_PASS : (g + 1) * K_PASS, :]

@@ -20,7 +20,12 @@ PACK = 4
 K_PASS = P * PACK
 PASSES = K // K_PASS
 LIST_ROWS = 16
+QUADRANTS, QUADRANT = 4, 32
+HALF = S // 2
+W_BYTES = PACK * M * 4
+WINDOW_BYTES = T * 4
 SPLIT = 384
+CHUNK = 256
 
 
 def tile_picked_zmae_lingelu_po_kernel(
@@ -45,7 +50,7 @@ def tile_picked_zmae_lingelu_po_kernel(
         nc.scalar.activation(warm[:, 1:2], warm[:, 0:1], GELU)
 
         def load_w(g):
-            raw = reused.tile([P, PACK, M], F32, name=f"w_raw{g}", align_bytes=64, offset=8192 * g)
+            raw = reused.tile([P, PACK, M], F32, name=f"w_raw{g}", align_bytes=64, offset=W_BYTES * g)
             rows = w1[g * K_PASS : (g + 1) * K_PASS, :]
             nc.sync.dma_start(raw[:], rows.rearrange("(p j) c -> p j c", j=PACK))
             return raw[:].rearrange("p j (m t) -> p m j t", t=PACK)
@@ -56,25 +61,26 @@ def tile_picked_zmae_lingelu_po_kernel(
             nc.sync.dma_start(table[:].bitcast(I32), words_in)
             return table
 
-        def rows_of(dram, t):
+        def plane_of(dram, t):
             return dram.rearrange("(p t) c -> p t c", t=PACK)[:, t, :]
 
         def load_window(t):
             if t % 2 == 0:
                 window = keep.tile([P, T], F32, name=f"window{t}", align_bytes=64)
-                nc.sync.dma_start(window[:], rows_of(mask, t))
+                nc.sync.dma_start(window[:], plane_of(mask, t))
             else:
-                window = reused.tile([P, T], F32, name=f"window{t}", align_bytes=64, offset=8192 + 4096 * (t // 2))
-                nc.scalar.dma_start(window[:], rows_of(mask, t))
+                at = W_BYTES * (PASSES - 1) + WINDOW_BYTES * (t // 2)
+                window = reused.tile([P, T], F32, name=f"window{t}", align_bytes=64, offset=at)
+                nc.scalar.dma_start(window[:], plane_of(mask, t))
             return window
 
-        x0 = load_x(0)
+        word_table0 = load_x(0)
         nc.sync.dma_start(offsets[:], offs)
-        for q in range(4):
-            live = slice(32 * q, 32 * q + 4 * PASSES)
+        for q in range(QUADRANTS):
+            live = slice(QUADRANT * q, QUADRANT * q + 4 * PASSES)
             nc.sync.dma_start(scale_table[live, :].bitcast(I32), x_scales[:, 4 * q : 4 * q + 4, :].bitcast(I32))
         w_raw = [load_w(g) for g in range(PASSES)]
-        x1 = load_x(1)
+        word_table1 = load_x(1)
         windows = {t: load_window(t) for t in (0, 2)}
 
         def round_w(copy, g, h):
@@ -90,42 +96,39 @@ def tile_picked_zmae_lingelu_po_kernel(
 
         x_codes = [keep.tile([P, S], U32, name=f"x_codes{g}", align_bytes=64) for g in range(PASSES)]
         x_bytes = keep.tile([P, S], U8, name="x_bytes", align_bytes=64)
-        half = S // 2
-        slices = ((0, half), (half, S))
+        halves = ((0, HALF), (HALF, S))
         weights = {}
 
-        def products(name, parts):
-            width = sum(b - a for t, a, b in parts)
-            acc = psum.tile([P, width], F32, name=f"acc_{name}")
+        def products(name, planes, a, b):
+            width = b - a
+            acc = psum.tile([P, len(planes) * width], F32, name=f"acc_{name}")
             for g in range(PASSES):
-                at = 0
-                for n, (t, a, b) in enumerate(parts):
+                for n, t in enumerate(planes):
                     codes, scales = weights[g, t // 2]
                     cols = slice(t % 2 * P, (t % 2 + 1) * P)
                     nc.tensor.matmul_mx(
-                        out=acc[:, at : at + b - a],
+                        out=acc[:, n * width : (n + 1) * width],
                         lhsT=codes[:, cols].bitcast(FP8X4),
                         lhsT_scale=scales[:, cols],
                         rhs=x_codes[g][:, a:b].bitcast(FP8X4),
                         rhs_scale=x_bytes[4 * g : P, a:b],
                         start=(g == 0 and n == 0),
-                        stop=(g == PASSES - 1 and n == len(parts) - 1),
+                        stop=(g == PASSES - 1 and n == len(planes) - 1),
                     )
-                    at = at + b - a
-            y = keep.tile([P, width], F32, name=f"y_{name}", tag=f"y_{name}", align_bytes=64)
+            y = keep.tile([P, len(planes) * width], F32, name=f"y_{name}", align_bytes=64)
             nc.scalar.activation(y[:], acc[:], GELU)
-            return y
+            return {(t, a): y[:, n * width : (n + 1) * width] for n, t in enumerate(planes)}
 
-        def scatter(t, a, b, y):
+        def scatter(t, a, b, values):
             window = windows[t][:].indirect(picks(a, b))
             if t < 2:
-                nc.vector.tensor_copy(window, y)
+                nc.vector.tensor_copy(window, values)
             else:
-                nc.scalar.activation(window, y, COPY)
+                nc.scalar.activation(window, values, COPY)
             if b == S:
-                nc.sync.dma_start(rows_of(out_0, t), windows[t][:])
+                nc.sync.dma_start(plane_of(out_0, t), windows[t][:])
 
-        nc.vector.tensor_copy(x_codes[0][:], x0[:].indirect(offsets[:]))
+        nc.vector.tensor_copy(x_codes[0][:], word_table0[:].indirect(offsets[:]))
         nc.vector.tensor_copy(x_bytes[:], scale_table[:].indirect(offsets[:]))
         first = [round_w(nc.vector.tensor_copy, 0, 0), round_w(nc.scalar.copy, 0, 1)]
         for h in range(2):
@@ -133,63 +136,68 @@ def tile_picked_zmae_lingelu_po_kernel(
         second = [round_w(nc.vector.tensor_copy, 1, 0), round_w(nc.scalar.copy, 1, 1)]
         windows.update({t: load_window(t) for t in (1, 3)})
         weights[1, 0] = quantize_w(1, 0, second[0])
-        for a, b in slices:
-            nc.vector.tensor_copy(x_codes[1][:, a:b], x1[:].indirect(picks(a, b)))
-            if b == half:
+        for a, b in halves:
+            nc.vector.tensor_copy(x_codes[1][:, a:b], word_table1[:].indirect(picks(a, b)))
+            if b == HALF:
                 weights[1, 1] = quantize_w(1, 1, second[1])
-        lead = [products(f"lead{t}", [(t, 0, half)]) for t in range(2)]
-        front = products("front", [(2, 0, half), (3, 0, half)])
-        rest = products("rest", [(0, half, S), (1, half, S)])
-        back = products("back", [(2, half, S), (3, half, S)])
-        for t in range(2):
-            scatter(t, 0, half, lead[t][:])
-        for t in range(2):
-            scatter(t, half, S, rest[:, t * half : (t + 1) * half])
-        for t in range(2):
-            scatter(2 + t, 0, half, front[:, t * half : (t + 1) * half])
-        for t in range(2):
-            scatter(2 + t, half, S, back[:, t * half : (t + 1) * half])
 
-        spans = ((0, SPLIT), (SPLIT, T))
-        pairs = [
-            keep.tile([P, 2, b - a, 2], BF16, name=f"pairs{n}", align_bytes=64)
-            for n, (a, b) in enumerate(spans)
-        ]
+        ys = {}
+        for t in range(2):
+            ys.update(products(f"lead{t}", [t], 0, HALF))
+        ys.update(products("front", [2, 3], 0, HALF))
+        ys.update(products("rest", [0, 1], HALF, S))
+        ys.update(products("back", [2, 3], HALF, S))
+        for planes in ((0, 1), (2, 3)):
+            for a, b in halves:
+                for t in planes:
+                    scatter(t, a, b, ys[t, a])
 
-        def round_plane(copy, t, n):
-            a, b = spans[n]
-            copy(pairs[n][:, t // 2, :, t % 2], windows[t][:, a:b])
+        scalar_span, vector_span = (0, SPLIT), (SPLIT, T)
+        pairs = keep.tile([P, 2, T, 2], BF16, name="pairs", align_bytes=64)
+        scalar_pieces = ((0, CHUNK), (CHUNK, SPLIT))
+        vector_pieces = ((T - CHUNK, T), (SPLIT, T - CHUNK))
 
-        for n in range(2):
-            round_plane(nc.vector.tensor_copy, 0, n)
-        for n in range(2):
-            round_plane(nc.vector.tensor_copy, 1, n)
-        round_plane(nc.vector.tensor_copy, 2, 1)
-        round_plane(nc.scalar.copy, 2, 0)
-        round_plane(nc.scalar.copy, 3, 0)
-        round_plane(nc.vector.tensor_copy, 3, 1)
+        def round_plane(copy, t, a, b):
+            copy(pairs[:, t // 2, a:b, t % 2], windows[t][:, a:b])
 
-        out_codes = keep.tile([P, T], U32, name="out_codes", align_bytes=64)
-        out_scales = keep.tile([P, T], U8, name="out_scales", align_bytes=64)
-        words = out_1[0].rearrange("p n t -> p (n t)").bitcast(I32)
-        pieces = ((0, 0, 256), (0, 256, SPLIT), (1, SPLIT, 512), (1, 512, 768), (1, 768, T))
-        woven = {}
-        for n, a, b in pieces:
-            woven[a] = keep.tile([P, (b - a) * PACK], BF16, name=f"woven{a}", align_bytes=64)
-            dst = woven[a][:].rearrange("p (c u e) -> p c u e", u=2, e=2)
-            both = pairs[n][:].rearrange("p u c e -> p c u e")[:, a - spans[n][0] : b - spans[n][0]]
-            if n == 1:
+        for t in range(2):
+            round_plane(nc.vector.tensor_copy, t, 0, T)
+        round_plane(nc.vector.tensor_copy, 2, *vector_span)
+        for t in (2, 3):
+            round_plane(nc.scalar.copy, t, *scalar_span)
+        for a, b in vector_pieces:
+            round_plane(nc.vector.tensor_copy, 3, a, b)
+
+        def weave(a, b):
+            piece = keep.tile([P, (b - a) * PACK], BF16, name=f"woven{a}", align_bytes=64)
+            dst = piece[:].rearrange("p (c u e) -> p c u e", u=2, e=2)
+            both = pairs[:].rearrange("p u c e -> p c u e")[:, a:b]
+            if a >= SPLIT:
                 nc.vector.tensor_copy(dst, both)
             else:
                 nc.scalar.copy(dst.bitcast(F32), both.bitcast(F32))
-        for a, b in ((512, 768), (768, T), (SPLIT, 512), (0, 256), (256, SPLIT)):
+            return piece
+
+        out_codes = keep.tile([P, T], U32, name="out_codes", align_bytes=64)
+        out_scales = keep.tile([P, T], U8, name="out_scales", align_bytes=64)
+        words_out = out_1[0].rearrange("p n t -> p (n t)").bitcast(I32)
+        woven = {a: weave(a, b) for a, b in scalar_pieces + vector_pieces}
+
+        def quantize_out(a, b):
             nc.vector.quantize_mx(out=out_codes[:, a:b].bitcast(FP8X4), scales=out_scales[:, a:b], in_=woven[a][:])
-            if b == T:
-                nc.sync.dma_start(words[:, 512:], out_codes[:, 512:].bitcast(I32))
-        nc.sync.dma_start(words[:, :512], out_codes[:, :512].bitcast(I32))
-        for q in range(4):
+
+        def store_words(a, b):
+            nc.sync.dma_start(words_out[:, a:b], out_codes[:, a:b].bitcast(I32))
+
+        for a, b in vector_pieces:
+            quantize_out(a, b)
+        store_words(*vector_span)
+        for a, b in scalar_pieces:
+            quantize_out(a, b)
+            store_words(a, b)
+        for q in range(QUADRANTS):
             queue = nc.sync if q % 2 == 0 else nc.scalar
             queue.dma_start(
                 out_2[0, 4 * q : 4 * q + 4, :].bitcast(I32),
-                out_scales[32 * q : 32 * q + 4, :].bitcast(I32),
+                out_scales[QUADRANT * q : QUADRANT * q + 4, :].bitcast(I32),
             )

@@ -22,9 +22,9 @@ PASSES = K // K_PASS
 LIST_ROWS = 16
 QUADRANTS, QUADRANT = 4, 32
 HALF = S // 2
-W_BYTES = PACK * M * 4
-WINDOW_BYTES = T * 4
-SPLIT = 384
+LEAD = 128
+SPLIT = 528
+RELIEF = 96
 CHUNK = 256
 
 
@@ -34,7 +34,6 @@ def tile_picked_zmae_lingelu_po_kernel(
     nc = tc.nc
     with ExitStack() as ctx:
         keep = ctx.enter_context(tc.tile_pool(name="keep", bufs=1))
-        reused = ctx.enter_context(tc.tile_pool(name="reused", bufs=1))
         psum = ctx.enter_context(tc.psum_pool(name="psum", bufs=1))
 
         offsets = keep.tile([P, S // LIST_ROWS], U16, name="offsets")
@@ -50,7 +49,7 @@ def tile_picked_zmae_lingelu_po_kernel(
         nc.scalar.activation(warm[:, 1:2], warm[:, 0:1], GELU)
 
         def load_w(g):
-            raw = reused.tile([P, PACK, M], F32, name=f"w_raw{g}", align_bytes=64, offset=W_BYTES * g)
+            raw = keep.tile([P, PACK, M], F32, name=f"w_raw{g}", align_bytes=64)
             rows = w1[g * K_PASS : (g + 1) * K_PASS, :]
             nc.sync.dma_start(raw[:], rows.rearrange("(p j) c -> p j c", j=PACK))
             return raw[:].rearrange("p j (m t) -> p m j t", t=PACK)
@@ -65,13 +64,8 @@ def tile_picked_zmae_lingelu_po_kernel(
             return dram.rearrange("(p t) c -> p t c", t=PACK)[:, t, :]
 
         def load_window(t):
-            if t % 2 == 0:
-                window = keep.tile([P, T], F32, name=f"window{t}", align_bytes=64)
-                nc.sync.dma_start(window[:], plane_of(mask, t))
-            else:
-                at = W_BYTES * (PASSES - 1) + WINDOW_BYTES * (t // 2)
-                window = reused.tile([P, T], F32, name=f"window{t}", align_bytes=64, offset=at)
-                nc.scalar.dma_start(window[:], plane_of(mask, t))
+            window = keep.tile([P, T], F32, name=f"window{t}", align_bytes=64)
+            nc.sync.dma_start(window[:], plane_of(mask, t))
             return window
 
         word_table0 = load_x(0)
@@ -81,7 +75,7 @@ def tile_picked_zmae_lingelu_po_kernel(
             nc.sync.dma_start(scale_table[live, :].bitcast(I32), x_scales[:, 4 * q : 4 * q + 4, :].bitcast(I32))
         w_raw = [load_w(g) for g in range(PASSES)]
         word_table1 = load_x(1)
-        windows = {t: load_window(t) for t in (0, 2)}
+        windows = {t: load_window(t) for t in (1, 3, 0, 2)}
 
         def round_w(copy, g, h):
             rounded = keep.tile([P, 2 * K_PASS], BF16, name=f"w_bf{g}_{h}", align_bytes=64)
@@ -96,36 +90,34 @@ def tile_picked_zmae_lingelu_po_kernel(
 
         x_codes = [keep.tile([P, S], U32, name=f"x_codes{g}", align_bytes=64) for g in range(PASSES)]
         x_bytes = keep.tile([P, S], U8, name="x_bytes", align_bytes=64)
-        halves = ((0, HALF), (HALF, S))
         weights = {}
 
-        def products(name, planes, a, b):
-            width = b - a
-            acc = psum.tile([P, len(planes) * width], F32, name=f"acc_{name}")
+        def product(bank, parts, y):
+            acc = psum.tile([P, sum(b - a for t, a, b in parts)], F32, name=f"acc_{bank}")
             for g in range(PASSES):
-                for n, t in enumerate(planes):
+                at = 0
+                for n, (t, a, b) in enumerate(parts):
                     codes, scales = weights[g, t // 2]
                     cols = slice(t % 2 * P, (t % 2 + 1) * P)
                     nc.tensor.matmul_mx(
-                        out=acc[:, n * width : (n + 1) * width],
+                        out=acc[:, at : at + b - a],
                         lhsT=codes[:, cols].bitcast(FP8X4),
                         lhsT_scale=scales[:, cols],
                         rhs=x_codes[g][:, a:b].bitcast(FP8X4),
                         rhs_scale=x_bytes[4 * g : P, a:b],
                         start=(g == 0 and n == 0),
-                        stop=(g == PASSES - 1 and n == len(planes) - 1),
+                        stop=(g == PASSES - 1 and n == len(parts) - 1),
                     )
-            y = keep.tile([P, len(planes) * width], F32, name=f"y_{name}", align_bytes=64)
-            nc.scalar.activation(y[:], acc[:], GELU)
-            return {(t, a): y[:, n * width : (n + 1) * width] for n, t in enumerate(planes)}
+                    at = at + b - a
+            nc.scalar.activation(y, acc[:].rearrange("p (n c) -> p n c", n=len(parts)), GELU)
 
-        def scatter(t, a, b, values):
+        def scatter(engine, t, a, b, values, last=True):
             window = windows[t][:].indirect(picks(a, b))
-            if t < 2:
+            if engine == "vector":
                 nc.vector.tensor_copy(window, values)
             else:
                 nc.scalar.activation(window, values, COPY)
-            if b == S:
+            if last:
                 nc.sync.dma_start(plane_of(out_0, t), windows[t][:])
 
         nc.vector.tensor_copy(x_codes[0][:], word_table0[:].indirect(offsets[:]))
@@ -134,66 +126,89 @@ def tile_picked_zmae_lingelu_po_kernel(
         for h in range(2):
             weights[0, h] = quantize_w(0, h, first[h])
         second = [round_w(nc.vector.tensor_copy, 1, 0), round_w(nc.scalar.copy, 1, 1)]
-        windows.update({t: load_window(t) for t in (1, 3)})
         weights[1, 0] = quantize_w(1, 0, second[0])
-        for a, b in halves:
+        for a, b in ((0, LEAD), (LEAD, HALF), (HALF, S)):
             nc.vector.tensor_copy(x_codes[1][:, a:b], word_table1[:].indirect(picks(a, b)))
-            if b == HALF:
+            if a == 0:
                 weights[1, 1] = quantize_w(1, 1, second[1])
 
-        ys = {}
-        for t in range(2):
-            ys.update(products(f"lead{t}", [t], 0, HALF))
-        ys.update(products("front", [2, 3], 0, HALF))
-        ys.update(products("rest", [0, 1], HALF, S))
-        ys.update(products("back", [2, 3], HALF, S))
-        for planes in ((0, 1), (2, 3)):
-            for a, b in halves:
-                for t in planes:
-                    scatter(t, a, b, ys[t, a])
+        pair_row = keep.tile([P, 4 * T], BF16, name="pair_row", align_bytes=64)
+        pairs = pair_row[:, 0 : 4 * T].rearrange("p (u c e) -> p u c e", u=2, e=2)
 
-        scalar_span, vector_span = (0, SPLIT), (SPLIT, T)
-        pairs = keep.tile([P, 2, T, 2], BF16, name="pairs", align_bytes=64)
-        scalar_pieces = ((0, CHUNK), (CHUNK, SPLIT))
-        vector_pieces = ((T - CHUNK, T), (SPLIT, T - CHUNK))
+        one = pair_row[:, 2 * (T + SPLIT) : 2 * (T + SPLIT + 1)].bitcast(F32)
+        nc.vector.memset(one, 1.0)
+
+        def round_on_gpsimd(t):
+            nc.gpsimd.tensor_scalar(
+                pairs[:, t // 2, RELIEF:T, t % 2], windows[t][:, RELIEF:T], one, -0.0, mybir.AluOpType.mult, mybir.AluOpType.add
+            )
+
+        order = (2, 3, 0, 1)
+        ys = keep.tile([P, PACK, S], F32, name="ys", align_bytes=64)
+
+        def products(bank, first, end, a, b):
+            product(bank, [(t, a, b) for t in order[first:end]], ys[:, first:end, a:b])
+
+        def values(t, a, b):
+            return ys[:, order.index(t), a:b]
+
+        products("lead1", 3, 4, 0, LEAD)
+        products("lead", 0, 3, 0, LEAD)
+        products("second", 0, 4, LEAD, HALF)
+        products("back0", 2, 3, HALF, S)
+        products("back1", 3, 4, HALF, S)
+        products("back3", 1, 2, HALF, S)
+        scatter("vector", 1, 0, LEAD, values(1, 0, LEAD), last=False)
+        scatter("vector", 3, 0, LEAD, values(3, 0, LEAD), last=False)
+        scatter("vector", 0, 0, S, values(0, 0, S))
+        scatter("scalar", 1, LEAD, S, values(1, LEAD, S))
+        products("back2", 0, 1, HALF, S)
+        scatter("scalar", 3, LEAD, S, values(3, LEAD, S))
+        scatter("vector", 2, 0, S, values(2, 0, S))
+        for t in (1, 0):
+            round_on_gpsimd(t)
+
+        quantised = ((768, T), (384, 768), (128, 384), (0, 128))
+        scalar_pieces = ((320, SPLIT), (128, 320), (0, 128))
+        vector_pieces = ((768, T), (SPLIT, 768))
 
         def round_plane(copy, t, a, b):
             copy(pairs[:, t // 2, a:b, t % 2], windows[t][:, a:b])
 
-        for t in range(2):
-            round_plane(nc.vector.tensor_copy, t, 0, T)
-        round_plane(nc.vector.tensor_copy, 2, *vector_span)
-        for t in (2, 3):
-            round_plane(nc.scalar.copy, t, *scalar_span)
+        round_plane(nc.scalar.copy, 3, 0, SPLIT)
+        for t in (1, 0):
+            round_plane(nc.scalar.copy, t, 0, RELIEF)
+        for a, b in scalar_pieces:
+            round_plane(nc.scalar.copy, 2, a, b)
+        round_plane(nc.vector.tensor_copy, 3, SPLIT, T)
         for a, b in vector_pieces:
-            round_plane(nc.vector.tensor_copy, 3, a, b)
+            round_plane(nc.vector.tensor_copy, 2, a, b)
+
+        woven = keep.tile([P, T * PACK], BF16, name="woven", align_bytes=64)
 
         def weave(a, b):
-            piece = keep.tile([P, (b - a) * PACK], BF16, name=f"woven{a}", align_bytes=64)
-            dst = piece[:].rearrange("p (c u e) -> p c u e", u=2, e=2)
-            both = pairs[:].rearrange("p u c e -> p c u e")[:, a:b]
+            dst = woven[:, a * PACK : b * PACK].bitcast(F32).rearrange("p (c i u) -> p c u i", u=2, i=4)
+            both = pair_row[:].bitcast(F32).rearrange("p (u c i) -> p c u i", u=2, i=4)[:, a // 4 : b // 4]
             if a >= SPLIT:
                 nc.vector.tensor_copy(dst, both)
             else:
-                nc.scalar.copy(dst.bitcast(F32), both.bitcast(F32))
-            return piece
+                nc.scalar.copy(dst, both)
+
+        for a, b in scalar_pieces + vector_pieces:
+            weave(a, b)
 
         out_codes = keep.tile([P, T], U32, name="out_codes", align_bytes=64)
         out_scales = keep.tile([P, T], U8, name="out_scales", align_bytes=64)
         words_out = out_1[0].rearrange("p n t -> p (n t)").bitcast(I32)
-        woven = {a: weave(a, b) for a, b in scalar_pieces + vector_pieces}
-
-        def quantize_out(a, b):
-            nc.vector.quantize_mx(out=out_codes[:, a:b].bitcast(FP8X4), scales=out_scales[:, a:b], in_=woven[a][:])
 
         def store_words(a, b):
             nc.sync.dma_start(words_out[:, a:b], out_codes[:, a:b].bitcast(I32))
 
-        for a, b in vector_pieces:
-            quantize_out(a, b)
-        store_words(*vector_span)
-        for a, b in scalar_pieces:
-            quantize_out(a, b)
+        for a, b in quantised:
+            nc.vector.quantize_mx(
+                out=out_codes[:, a:b].bitcast(FP8X4), scales=out_scales[:, a:b], in_=woven[:, a * PACK : b * PACK]
+            )
+        for a, b in ((768, T), (384, 768), (0, 384)):
             store_words(a, b)
         for q in range(QUADRANTS):
             queue = nc.sync if q % 2 == 0 else nc.scalar

@@ -14,6 +14,7 @@ U8 = mybir.dt.uint8
 FP8X4 = mybir.dt.float8_e4m3fn_x4
 GELU = mybir.ActivationFunctionType.Gelu_apprx_tanh
 COPY = mybir.ActivationFunctionType.Copy
+MULT, ADD = mybir.AluOpType.mult, mybir.AluOpType.add
 
 P = 128
 PACK = 4
@@ -21,11 +22,17 @@ K_PASS = P * PACK
 PASSES = K // K_PASS
 LIST_ROWS = 16
 QUADRANTS, QUADRANT = 4, 32
+SCALE_ROWS = 4
+LINE = 4
 HALF = S // 2
 LEAD = 128
 SPLIT = 528
 RELIEF = 96
-CHUNK = 256
+SHARE = 96
+VECTOR_PIECES = ((768, T), (SPLIT, 768))
+SCALAR_PIECES = ((320, SPLIT), (128, 320), (0, 128))
+QUANTISED = ((768, T), (384, 768), (128, 384), (0, 128))
+STORED = ((768, T), (384, 768), (0, 384))
 
 
 def tile_picked_zmae_lingelu_po_kernel(
@@ -34,6 +41,7 @@ def tile_picked_zmae_lingelu_po_kernel(
     nc = tc.nc
     with ExitStack() as ctx:
         keep = ctx.enter_context(tc.tile_pool(name="keep", bufs=1))
+        reused = ctx.enter_context(tc.tile_pool(name="reused", bufs=1))
         psum = ctx.enter_context(tc.psum_pool(name="psum", bufs=1))
 
         offsets = keep.tile([P, S // LIST_ROWS], U16, name="offsets")
@@ -49,7 +57,7 @@ def tile_picked_zmae_lingelu_po_kernel(
         nc.scalar.activation(warm[:, 1:2], warm[:, 0:1], GELU)
 
         def load_w(g):
-            raw = keep.tile([P, PACK, M], F32, name=f"w_raw{g}", align_bytes=64)
+            raw = reused.tile([P, PACK, M], F32, name=f"w_raw{g}", align_bytes=64, offset=PACK * M * 4 * g)
             rows = w1[g * K_PASS : (g + 1) * K_PASS, :]
             nc.sync.dma_start(raw[:], rows.rearrange("(p j) c -> p j c", j=PACK))
             return raw[:].rearrange("p j (m t) -> p m j t", t=PACK)
@@ -71,8 +79,9 @@ def tile_picked_zmae_lingelu_po_kernel(
         word_table0 = load_x(0)
         nc.sync.dma_start(offsets[:], offs)
         for q in range(QUADRANTS):
-            live = slice(QUADRANT * q, QUADRANT * q + 4 * PASSES)
-            nc.sync.dma_start(scale_table[live, :].bitcast(I32), x_scales[:, 4 * q : 4 * q + 4, :].bitcast(I32))
+            live = slice(QUADRANT * q, QUADRANT * q + SCALE_ROWS * PASSES)
+            rows = x_scales[:, SCALE_ROWS * q : SCALE_ROWS * (q + 1), :]
+            nc.sync.dma_start(scale_table[live, :].bitcast(I32), rows.bitcast(I32))
         w_raw = [load_w(g) for g in range(PASSES)]
         word_table1 = load_x(1)
         windows = {t: load_window(t) for t in (1, 3, 0, 2)}
@@ -88,36 +97,44 @@ def tile_picked_zmae_lingelu_po_kernel(
             nc.vector.quantize_mx(out=codes[:].bitcast(FP8X4), scales=scales[:], in_=rounded[:])
             return codes, scales
 
-        x_codes = [keep.tile([P, S], U32, name=f"x_codes{g}", align_bytes=64) for g in range(PASSES)]
+        x_codes = [keep.tile([P, S // (g + 1)], U32, name=f"x_codes{g}", align_bytes=64) for g in range(PASSES)]
+        x_last = reused.tile([P, HALF], U32, name="x_last", align_bytes=64, offset=PACK * M * 4)
+
+        def x_words_at(g, a, b):
+            return x_last[:] if (g, a) == (1, HALF) else x_codes[g][:, a:b]
+
         x_bytes = keep.tile([P, S], U8, name="x_bytes", align_bytes=64)
         weights = {}
 
-        def product(bank, parts, y):
-            acc = psum.tile([P, sum(b - a for t, a, b in parts)], F32, name=f"acc_{bank}")
+        order = (2, 3, 0, 1)
+        ys = keep.tile([P, PACK, S], F32, name="ys", align_bytes=64)
+
+        def products(planes, a, b):
+            acc = psum.tile([P, len(planes), b - a], F32, name=f"acc{planes[0]}_{a}")
             for g in range(PASSES):
-                at = 0
-                for n, (t, a, b) in enumerate(parts):
+                for n, t in enumerate(planes):
                     codes, scales = weights[g, t // 2]
                     cols = slice(t % 2 * P, (t % 2 + 1) * P)
                     nc.tensor.matmul_mx(
-                        out=acc[:, at : at + b - a],
+                        out=acc[:, n, :],
                         lhsT=codes[:, cols].bitcast(FP8X4),
                         lhsT_scale=scales[:, cols],
-                        rhs=x_codes[g][:, a:b].bitcast(FP8X4),
-                        rhs_scale=x_bytes[4 * g : P, a:b],
+                        rhs=x_words_at(g, a, b).bitcast(FP8X4),
+                        rhs_scale=x_bytes[SCALE_ROWS * g : P, a:b],
                         start=(g == 0 and n == 0),
-                        stop=(g == PASSES - 1 and n == len(parts) - 1),
+                        stop=(g == PASSES - 1 and n == len(planes) - 1),
                     )
-                    at = at + b - a
-            nc.scalar.activation(y, acc[:].rearrange("p (n c) -> p n c", n=len(parts)), GELU)
+            at = order.index(planes[0])
+            nc.scalar.activation(ys[:, at : at + len(planes), a:b], acc[:], GELU)
 
-        def scatter(engine, t, a, b, values, last=True):
+        def scatter(t, a, b):
             window = windows[t][:].indirect(picks(a, b))
-            if engine == "vector":
+            values = ys[:, order.index(t), a:b]
+            if a == 0:
                 nc.vector.tensor_copy(window, values)
             else:
                 nc.scalar.activation(window, values, COPY)
-            if last:
+            if b == S:
                 nc.sync.dma_start(plane_of(out_0, t), windows[t][:])
 
         nc.vector.tensor_copy(x_codes[0][:], word_table0[:].indirect(offsets[:]))
@@ -125,52 +142,37 @@ def tile_picked_zmae_lingelu_po_kernel(
         first = [round_w(nc.vector.tensor_copy, 0, 0), round_w(nc.scalar.copy, 0, 1)]
         for h in range(2):
             weights[0, h] = quantize_w(0, h, first[h])
-        second = [round_w(nc.vector.tensor_copy, 1, 0), round_w(nc.scalar.copy, 1, 1)]
+        lead_bf = keep.tile([P, 2 * K_PASS], BF16, name="w_bf1_0", align_bytes=64)
+        dealt = lead_bf[:].rearrange("p (t m j) -> p m j t", t=2, j=PACK)
+        nc.vector.tensor_copy(dealt[:, 0:SHARE], w_raw[1][:, 0:SHARE, :, 0:2])
+        nc.scalar.copy(dealt[:, SHARE:P], w_raw[1][:, SHARE:P, :, 0:2])
+        second = [lead_bf, round_w(nc.scalar.copy, 1, 1)]
         weights[1, 0] = quantize_w(1, 0, second[0])
         for a, b in ((0, LEAD), (LEAD, HALF), (HALF, S)):
-            nc.vector.tensor_copy(x_codes[1][:, a:b], word_table1[:].indirect(picks(a, b)))
-            if a == 0:
+            nc.vector.tensor_copy(x_words_at(1, a, b), word_table1[:].indirect(picks(a, b)))
+            if a == LEAD:
                 weights[1, 1] = quantize_w(1, 1, second[1])
 
-        pair_row = keep.tile([P, 4 * T], BF16, name="pair_row", align_bytes=64)
-        pairs = pair_row[:, 0 : 4 * T].rearrange("p (u c e) -> p u c e", u=2, e=2)
+        pair_row = keep.tile([P, PACK * T], BF16, name="pair_row", align_bytes=64)
+        pairs = pair_row[:].rearrange("p (u c e) -> p u c e", u=2, e=2)
 
         one = pair_row[:, 2 * (T + SPLIT) : 2 * (T + SPLIT + 1)].bitcast(F32)
         nc.vector.memset(one, 1.0)
 
-        def round_on_gpsimd(t):
-            nc.gpsimd.tensor_scalar(
-                pairs[:, t // 2, RELIEF:T, t % 2], windows[t][:, RELIEF:T], one, -0.0, mybir.AluOpType.mult, mybir.AluOpType.add
-            )
-
-        order = (2, 3, 0, 1)
-        ys = keep.tile([P, PACK, S], F32, name="ys", align_bytes=64)
-
-        def products(bank, first, end, a, b):
-            product(bank, [(t, a, b) for t in order[first:end]], ys[:, first:end, a:b])
-
-        def values(t, a, b):
-            return ys[:, order.index(t), a:b]
-
-        products("lead1", 3, 4, 0, LEAD)
-        products("lead", 0, 3, 0, LEAD)
-        products("second", 0, 4, LEAD, HALF)
-        products("back0", 2, 3, HALF, S)
-        products("back1", 3, 4, HALF, S)
-        products("back3", 1, 2, HALF, S)
-        scatter("vector", 1, 0, LEAD, values(1, 0, LEAD), last=False)
-        scatter("vector", 3, 0, LEAD, values(3, 0, LEAD), last=False)
-        scatter("vector", 0, 0, S, values(0, 0, S))
-        scatter("scalar", 1, LEAD, S, values(1, LEAD, S))
-        products("back2", 0, 1, HALF, S)
-        scatter("scalar", 3, LEAD, S, values(3, LEAD, S))
-        scatter("vector", 2, 0, S, values(2, 0, S))
+        products((1,), 0, LEAD)
+        products((2, 3, 0), 0, LEAD)
+        products(order, LEAD, HALF)
+        for t in (0, 1, 3):
+            products((t,), HALF, S)
+        scatter(1, 0, LEAD)
+        scatter(3, 0, LEAD)
+        scatter(0, 0, S)
+        scatter(1, LEAD, S)
+        products((2,), HALF, S)
+        scatter(3, LEAD, S)
+        scatter(2, 0, S)
         for t in (1, 0):
-            round_on_gpsimd(t)
-
-        quantised = ((768, T), (384, 768), (128, 384), (0, 128))
-        scalar_pieces = ((320, SPLIT), (128, 320), (0, 128))
-        vector_pieces = ((768, T), (SPLIT, 768))
+            nc.gpsimd.tensor_scalar(pairs[:, 0, RELIEF:T, t], windows[t][:, RELIEF:T], one, -0.0, MULT, ADD)
 
         def round_plane(copy, t, a, b):
             copy(pairs[:, t // 2, a:b, t % 2], windows[t][:, a:b])
@@ -178,41 +180,37 @@ def tile_picked_zmae_lingelu_po_kernel(
         round_plane(nc.scalar.copy, 3, 0, SPLIT)
         for t in (1, 0):
             round_plane(nc.scalar.copy, t, 0, RELIEF)
-        for a, b in scalar_pieces:
+        for a, b in SCALAR_PIECES:
             round_plane(nc.scalar.copy, 2, a, b)
         round_plane(nc.vector.tensor_copy, 3, SPLIT, T)
-        for a, b in vector_pieces:
+        for a, b in VECTOR_PIECES:
             round_plane(nc.vector.tensor_copy, 2, a, b)
 
         woven = keep.tile([P, T * PACK], BF16, name="woven", align_bytes=64)
+        pair_words = pair_row[:].bitcast(F32).rearrange("p (u c i) -> p c u i", u=2, i=LINE)
 
-        def weave(a, b):
-            dst = woven[:, a * PACK : b * PACK].bitcast(F32).rearrange("p (c i u) -> p c u i", u=2, i=4)
-            both = pair_row[:].bitcast(F32).rearrange("p (u c i) -> p c u i", u=2, i=4)[:, a // 4 : b // 4]
-            if a >= SPLIT:
-                nc.vector.tensor_copy(dst, both)
-            else:
-                nc.scalar.copy(dst, both)
+        def weave(copy, a, b):
+            dst = woven[:, a * PACK : b * PACK].bitcast(F32).rearrange("p (c i u) -> p c u i", u=2, i=LINE)
+            copy(dst, pair_words[:, a // LINE : b // LINE])
 
-        for a, b in scalar_pieces + vector_pieces:
-            weave(a, b)
+        for a, b in SCALAR_PIECES:
+            weave(nc.scalar.copy, a, b)
+        for a, b in VECTOR_PIECES:
+            weave(nc.vector.tensor_copy, a, b)
 
         out_codes = keep.tile([P, T], U32, name="out_codes", align_bytes=64)
         out_scales = keep.tile([P, T], U8, name="out_scales", align_bytes=64)
         words_out = out_1[0].rearrange("p n t -> p (n t)").bitcast(I32)
 
-        def store_words(a, b):
-            nc.sync.dma_start(words_out[:, a:b], out_codes[:, a:b].bitcast(I32))
-
-        for a, b in quantised:
+        for a, b in QUANTISED:
             nc.vector.quantize_mx(
                 out=out_codes[:, a:b].bitcast(FP8X4), scales=out_scales[:, a:b], in_=woven[:, a * PACK : b * PACK]
             )
-        for a, b in ((768, T), (384, 768), (0, 384)):
-            store_words(a, b)
+        for a, b in STORED:
+            nc.sync.dma_start(words_out[:, a:b], out_codes[:, a:b].bitcast(I32))
         for q in range(QUADRANTS):
             queue = nc.sync if q % 2 == 0 else nc.scalar
             queue.dma_start(
-                out_2[0, 4 * q : 4 * q + 4, :].bitcast(I32),
-                out_scales[QUADRANT * q : QUADRANT * q + 4, :].bitcast(I32),
+                out_2[0, SCALE_ROWS * q : SCALE_ROWS * (q + 1), :].bitcast(I32),
+                out_scales[QUADRANT * q : QUADRANT * q + SCALE_ROWS, :].bitcast(I32),
             )

from contextlib import ExitStack

import concourse.mybir as mybir

K, T, S, M = 1024, 1024, 512, 512
FLOPS = 2 * K * S * M

F32 = mybir.dt.float32
BF16 = mybir.dt.bfloat16
I32 = mybir.dt.int32
U32 = mybir.dt.uint32
U16 = mybir.dt.uint16
U8 = mybir.dt.uint8
FP8X4 = mybir.dt.float8_e4m3fn_x4
GELU = mybir.ActivationFunctionType.Gelu_apprx_tanh
COPY = mybir.ActivationFunctionType.Copy
MULT, ADD = mybir.AluOpType.mult, mybir.AluOpType.add

P = 128
PACK = 4
K_PASS = P * PACK
PASSES = K // K_PASS
LIST_ROWS = 16
QUADRANTS, QUADRANT = 4, 32
SCALE_ROWS = 4
LINE = 4
HALF = S // 2
LEAD = 128
SPLIT = 528
RELIEF = 96
SHARE = 96
VECTOR_PIECES = ((768, T), (SPLIT, 768))
SCALAR_PIECES = ((320, SPLIT), (128, 320), (0, 128))
QUANTISED = ((768, T), (384, 768), (128, 384), (0, 128))
STORED = ((768, T), (384, 768), (0, 384))


def tile_picked_zmae_lingelu_po_kernel(
    tc, x_words, x_scales, mask, w1, offs, out_0, out_1, out_2
):
    nc = tc.nc
    with ExitStack() as ctx:
        keep = ctx.enter_context(tc.tile_pool(name="keep", bufs=1))
        reused = ctx.enter_context(tc.tile_pool(name="reused", bufs=1))
        psum = ctx.enter_context(tc.psum_pool(name="psum", bufs=1))

        offsets = keep.tile([P, S // LIST_ROWS], U16, name="offsets")

        def picks(a, b):
            return offsets[:, a // LIST_ROWS : b // LIST_ROWS]

        scale_table = keep.tile([P, T], U8, name="scale_table", align_bytes=64)
        nc.gpsimd.memset(scale_table[:].bitcast(I32), 0)

        warm = keep.tile([P, 2], F32, name="warm")
        nc.vector.memset(warm[:], 0.0)
        nc.scalar.activation(warm[:, 1:2], warm[:, 0:1], GELU)

        def load_w(g):
            raw = reused.tile([P, PACK, M], F32, name=f"w_raw{g}", align_bytes=64, offset=PACK * M * 4 * g)
            rows = w1[g * K_PASS : (g + 1) * K_PASS, :]
            nc.sync.dma_start(raw[:], rows.rearrange("(p j) c -> p j c", j=PACK))
            return raw[:].rearrange("p j (m t) -> p m j t", t=PACK)

        def load_x(g):
            table = keep.tile([P, T], U32, name=f"word_table{g}", align_bytes=64)
            words_in = x_words[g].rearrange("p n t -> p (n t)").bitcast(I32)
            nc.sync.dma_start(table[:].bitcast(I32), words_in)
            return table

        def plane_of(dram, t):
            return dram.rearrange("(p t) c -> p t c", t=PACK)[:, t, :]

        def load_window(t):
            window = keep.tile([P, T], F32, name=f"window{t}", align_bytes=64)
            nc.sync.dma_start(window[:], plane_of(mask, t))
            return window

        word_table0 = load_x(0)
        nc.sync.dma_start(offsets[:], offs)
        for q in range(QUADRANTS):
            live = slice(QUADRANT * q, QUADRANT * q + SCALE_ROWS * PASSES)
            rows = x_scales[:, SCALE_ROWS * q : SCALE_ROWS * (q + 1), :]
            nc.sync.dma_start(scale_table[live, :].bitcast(I32), rows.bitcast(I32))
        w_raw = [load_w(g) for g in range(PASSES)]
        word_table1 = load_x(1)
        windows = {t: load_window(t) for t in (1, 3, 0, 2)}

        def round_w(copy, g, h):
            rounded = keep.tile([P, 2 * K_PASS], BF16, name=f"w_bf{g}_{h}", align_bytes=64)
            copy(rounded[:].rearrange("p (t m j) -> p m j t", t=2, j=PACK), w_raw[g][:, :, :, 2 * h : 2 * h + 2])
            return rounded

        def quantize_w(g, h, rounded):
            codes = keep.tile([P, 2 * P], U32, name=f"w_codes{g}_{h}", align_bytes=64)
            scales = keep.tile([P, 2 * P], U8, name=f"w_scales{g}_{h}", align_bytes=64)
            nc.vector.quantize_mx(out=codes[:].bitcast(FP8X4), scales=scales[:], in_=rounded[:])
            return codes, scales

        x_codes = [keep.tile([P, S // (g + 1)], U32, name=f"x_codes{g}", align_bytes=64) for g in range(PASSES)]
        x_last = reused.tile([P, HALF], U32, name="x_last", align_bytes=64, offset=PACK * M * 4)

        def x_words_at(g, a, b):
            return x_last[:] if (g, a) == (1, HALF) else x_codes[g][:, a:b]

        x_bytes = keep.tile([P, S], U8, name="x_bytes", align_bytes=64)
        weights = {}

        order = (2, 3, 0, 1)
        ys = keep.tile([P, PACK, S], F32, name="ys", align_bytes=64)

        def products(planes, a, b):
            acc = psum.tile([P, len(planes), b - a], F32, name=f"acc{planes[0]}_{a}")
            for g in range(PASSES):
                for n, t in enumerate(planes):
                    codes, scales = weights[g, t // 2]
                    cols = slice(t % 2 * P, (t % 2 + 1) * P)
                    nc.tensor.matmul_mx(
                        out=acc[:, n, :],
                        lhsT=codes[:, cols].bitcast(FP8X4),
                        lhsT_scale=scales[:, cols],
                        rhs=x_words_at(g, a, b).bitcast(FP8X4),
                        rhs_scale=x_bytes[SCALE_ROWS * g : P, a:b],
                        start=(g == 0 and n == 0),
                        stop=(g == PASSES - 1 and n == len(planes) - 1),
                    )
            at = order.index(planes[0])
            nc.scalar.activation(ys[:, at : at + len(planes), a:b], acc[:], GELU)

        def scatter(t, a, b):
            window = windows[t][:].indirect(picks(a, b))
            values = ys[:, order.index(t), a:b]
            if a == 0:
                nc.vector.tensor_copy(window, values)
            else:
                nc.scalar.activation(window, values, COPY)
            if b == S:
                nc.sync.dma_start(plane_of(out_0, t), windows[t][:])

        nc.vector.tensor_copy(x_codes[0][:], word_table0[:].indirect(offsets[:]))
        nc.vector.tensor_copy(x_bytes[:], scale_table[:].indirect(offsets[:]))
        first = [round_w(nc.vector.tensor_copy, 0, 0), round_w(nc.scalar.copy, 0, 1)]
        for h in range(2):
            weights[0, h] = quantize_w(0, h, first[h])
        lead_bf = keep.tile([P, 2 * K_PASS], BF16, name="w_bf1_0", align_bytes=64)
        dealt = lead_bf[:].rearrange("p (t m j) -> p m j t", t=2, j=PACK)
        nc.vector.tensor_copy(dealt[:, 0:SHARE], w_raw[1][:, 0:SHARE, :, 0:2])
        nc.scalar.copy(dealt[:, SHARE:P], w_raw[1][:, SHARE:P, :, 0:2])
        second = [lead_bf, round_w(nc.scalar.copy, 1, 1)]
        weights[1, 0] = quantize_w(1, 0, second[0])
        for a, b in ((0, LEAD), (LEAD, HALF), (HALF, S)):
            nc.vector.tensor_copy(x_words_at(1, a, b), word_table1[:].indirect(picks(a, b)))
            if a == LEAD:
                weights[1, 1] = quantize_w(1, 1, second[1])

        pair_row = keep.tile([P, PACK * T], BF16, name="pair_row", align_bytes=64)
        pairs = pair_row[:].rearrange("p (u c e) -> p u c e", u=2, e=2)

        one = pair_row[:, 2 * (T + SPLIT) : 2 * (T + SPLIT + 1)].bitcast(F32)
        nc.vector.memset(one, 1.0)

        products((1,), 0, LEAD)
        products((2, 3, 0), 0, LEAD)
        products(order, LEAD, HALF)
        for t in (0, 1, 3):
            products((t,), HALF, S)
        scatter(1, 0, LEAD)
        scatter(3, 0, LEAD)
        scatter(0, 0, S)
        scatter(1, LEAD, S)
        products((2,), HALF, S)
        scatter(3, LEAD, S)
        scatter(2, 0, S)
        for t in (1, 0):
            nc.gpsimd.tensor_scalar(pairs[:, 0, RELIEF:T, t], windows[t][:, RELIEF:T], one, -0.0, MULT, ADD)

        def round_plane(copy, t, a, b):
            copy(pairs[:, t // 2, a:b, t % 2], windows[t][:, a:b])

        round_plane(nc.scalar.copy, 3, 0, SPLIT)
        for t in (1, 0):
            round_plane(nc.scalar.copy, t, 0, RELIEF)
        for a, b in SCALAR_PIECES:
            round_plane(nc.scalar.copy, 2, a, b)
        round_plane(nc.vector.tensor_copy, 3, SPLIT, T)
        for a, b in VECTOR_PIECES:
            round_plane(nc.vector.tensor_copy, 2, a, b)

        woven = keep.tile([P, T * PACK], BF16, name="woven", align_bytes=64)
        pair_words = pair_row[:].bitcast(F32).rearrange("p (u c i) -> p c u i", u=2, i=LINE)

        def weave(copy, a, b):
            dst = woven[:, a * PACK : b * PACK].bitcast(F32).rearrange("p (c i u) -> p c u i", u=2, i=LINE)
            copy(dst, pair_words[:, a // LINE : b // LINE])

        for a, b in SCALAR_PIECES:
            weave(nc.scalar.copy, a, b)
        for a, b in VECTOR_PIECES:
            weave(nc.vector.tensor_copy, a, b)

        out_codes = keep.tile([P, T], U32, name="out_codes", align_bytes=64)
        out_scales = keep.tile([P, T], U8, name="out_scales", align_bytes=64)
        words_out = out_1[0].rearrange("p n t -> p (n t)").bitcast(I32)

        for a, b in QUANTISED:
            nc.vector.quantize_mx(
                out=out_codes[:, a:b].bitcast(FP8X4), scales=out_scales[:, a:b], in_=woven[:, a * PACK : b * PACK]
            )
        for a, b in STORED:
            nc.sync.dma_start(words_out[:, a:b], out_codes[:, a:b].bitcast(I32))
        for q in range(QUADRANTS):
            queue = nc.sync if q % 2 == 0 else nc.scalar
            queue.dma_start(
                out_2[0, SCALE_ROWS * q : SCALE_ROWS * (q + 1), :].bitcast(I32),
                out_scales[QUADRANT * q : QUADRANT * q + SCALE_ROWS, :].bitcast(I32),
            )
